import numpy as np
import ml_dtypes


def mxq(x, axis, fmt="e4m3"):
    dtype, down = {"e4m3": (ml_dtypes.float8_e4m3fn, 7), "e5m2": (ml_dtypes.float8_e5m2, 14)}[fmt]
    v = np.moveaxis(np.asarray(x, np.float32).astype(ml_dtypes.bfloat16).astype(np.float64), axis, -1)
    blocks = v.reshape(v.shape[:-1] + (-1, 32))
    amax = np.abs(blocks).max(-1, keepdims=True)
    byte = np.maximum(np.where(amax > 0, np.frexp(amax)[1] - 1 + 127, 0) - down, 1)
    scale = np.exp2(byte - 127.0)
    codes = (blocks / scale).astype(np.float32).astype(dtype).astype(np.float64)
    return np.moveaxis((codes * scale).reshape(v.shape), -1, axis)


WIDE = False


def mx_kscale(k):
    if not WIDE:
        return np.ones(k)
    levels = np.array([10, -10, 5, -5, 0])
    if k % 512:
        return np.exp2(np.random.permutation(np.resize(levels, k // 32))).repeat(32)
    a = np.empty((k // 512, 16))
    for p in range(k // 512):
        a[p, :8] = np.random.permutation(np.resize(levels, 8))
        for g in range(8):
            far = levels[np.abs(levels - a[p, g]) >= 10]
            a[p, g + 8] = far[np.random.randint(len(far))]
    return np.exp2(a.ravel()).repeat(32)


def f64(x):
    return np.asarray(x).astype(np.float64)


def striped(idx):
    return np.tile(idx.reshape(-1, 16).T, (8, 1)).astype(np.uint16)


def unstriped(offs):
    return offs[:16].T.reshape(-1).astype(np.int64)


def pack_weight(w):
    k, n = w.shape
    w = f64(np.asarray(w, np.float32).astype(ml_dtypes.bfloat16)).reshape(k // 32, 32, n)
    amax = np.abs(w).max(1)
    byte = np.clip(np.where(amax > 0, np.frexp(amax)[1] - 1 + 127 - 7, 1), 1, 254)
    scaled = (w * np.exp2(127.0 - byte)[:, None, :]).reshape(k, n).astype(np.float32)
    words = np.ascontiguousarray(scaled.reshape(k // 512, 128, 4, n).transpose(0, 1, 3, 2)).astype(ml_dtypes.float8_e4m3fn).view(np.uint8)
    return words, np.ascontiguousarray(byte.astype(np.uint8).reshape(k // 512, 16, n))


def unpack_weight(words, scales):
    g, p, n, _ = words.shape
    vals = np.ascontiguousarray(words).view(ml_dtypes.float8_e4m3fn).astype(np.float64) * np.repeat(np.exp2(scales.astype(np.float64) - 127.0), 8, axis=1)[..., None]
    return vals.transpose(0, 1, 3, 2).reshape(g * 512, n)


K, T, S, H, D, V, W, U = 512, 2048, 512, 512, 4, 128, 2048, 512
P = 2 ** 7


def setup_inputs():
    n = np.random.standard_normal
    s = mx_kscale(K)[:, None]
    u = mx_kscale(H)
    packed_xT = pack_weight(n((K, T)) * s)
    packed_eT = pack_weight(n((H, W)) / np.sqrt(H) / u[:, None])
    return {
        "x_words": packed_xT[0],
        "x_scales": packed_xT[1],
        "w1": (n((K, H)) / np.sqrt(K) / s * u).astype(np.float32),
        "e_words": packed_eT[0],
        "e_scales": packed_eT[1],
        "half": (np.tile(np.random.uniform(0.2, 1.0, W), (P, 1))).astype(np.float32),
        "prior": (np.tile(0.5 * n(V), (P, 1))).astype(np.float32),
        "offs": striped(np.random.permutation(T)[:S]),
        "pro": striped(np.random.permutation(W)[:U]),
    }


def reference(x_words, x_scales, w1, e_words, e_scales, half, prior, offs, pro):
    xq = unpack_weight(x_words, x_scales)[:, unstriped(offs)]
    h = mxq(f64(w1), 0, "e4m3").T @ xq
    e_pro = unpack_weight(e_words, e_scales)[:, unstriped(pro)]
    y = mxq(h, 0, "e4m3").T @ e_pro
    ee = np.exp(y - (f64(half)[:1][:, unstriped(pro)]))
    l = np.log(ee.reshape(len(ee), -1, D).sum(axis=2)) + f64(prior)[:1]
    ex = np.exp(l - l.max(axis=1, keepdims=True))
    return ex / ex.sum(axis=1, keepdims=True)

@@ -1,0 +1,209 @@
+from contextlib import ExitStack
+
+import concourse.mybir as mybir
+
+F32 = mybir.dt.float32
+BF16 = mybir.dt.bfloat16
+I32 = mybir.dt.int32
+U32 = mybir.dt.uint32
+U16 = mybir.dt.uint16
+U8 = mybir.dt.uint8
+FP8X4 = mybir.dt.float8_e4m3fn_x4
+ALU = mybir.AluOpType
+ACT = mybir.ActivationFunctionType
+AX = mybir.AxisListType
+
+P = 128
+PACK = 4
+TABLE = 2048
+S = 512
+H = 512
+U = 512
+D = 4
+V = 128
+HALF = 256
+ON_TENSOR = 2
+FLOPS = 2 * 512 * 512 * 512 * 2
+
+
+def tile_picked_yparz_post_p_kernel(
+    tc, x_words, x_scales, w1, e_words, e_scales, half, prior, offs, pro, out
+):
+    nc = tc.nc
+    with ExitStack() as ctx:
+        keep = ctx.enter_context(tc.tile_pool(name="keep", bufs=1))
+        tables = ctx.enter_context(tc.tile_pool(name="tables", bufs=1))
+        psum = ctx.enter_context(tc.psum_pool(name="psum", bufs=1))
+
+        offs_sb = keep.tile([P, S // 16], U16, name="offs_sb")
+        pro_sb = keep.tile([P, U // 16], U16, name="pro_sb")
+        xs_table = keep.tile([P, TABLE], U8, name="xs_table", tag="t1", align_bytes=64)
+        es_table = keep.tile([P, TABLE], U8, name="es_table", tag="t3", align_bytes=64)
+        half_table = keep.tile([P, TABLE], F32, name="half_table", tag="t2", align_bytes=64)
+        zeros = tables.tile([P, P], F32, name="zeros", offset=4 * TABLE - 256, align_bytes=64)
+        x_table = tables.tile([P, TABLE], U32, name="x_table", offset=0, align_bytes=64)
+        e_table = tables.tile([P, TABLE], U32, name="e_table", offset=4 * TABLE, align_bytes=64)
+        prior_sb = keep.tile([P, V], F32, name="prior_sb")
+        w_raw = [keep.tile([P, PACK, HALF], F32, name=f"w_raw{u}") for u in range(2)]
+
+        nc.vector.memset(xs_table[:].bitcast(I32), 0)
+        nc.vector.memset(es_table[:].bitcast(I32), 0)
+        nc.vector.memset(half_table[:], 0.0)
+        nc.vector.memset(zeros[:], 0.0)
+        ident = keep.tile([P, P], F32, name="ident")
+        nc.gpsimd.affine_select(
+            out=ident[:], in_=zeros[:], compare_op=ALU.not_equal, fill=1.0, base=0, pattern=[[-1, P]], channel_multiplier=1
+        )
+        nc.gpsimd.dma_start(prior_sb[:], prior)
+
+        w_rows = w1.rearrange("(p j) c -> p j c", j=PACK)
+        xs_rows = x_scales[0].rearrange("(q r) c -> r q c", r=4)
+        es_rows = e_scales[0].rearrange("(q r) c -> r q c", r=4)
+        nc.sync.dma_start(offs_sb[:], offs)
+        nc.sync.dma_start(pro_sb[:], pro)
+        for r in range(4):
+            nc.sync.dma_start(xs_table[r:P:32, :].bitcast(I32), xs_rows[r].bitcast(I32))
+        nc.sync.dma_start(w_raw[0][:], w_rows[:, :, :HALF])
+        nc.sync.dma_start(w_raw[1][:], w_rows[:, :, HALF:])
+        nc.sync.dma_start(half_table[0:1, :], half[0:1, :])
+        nc.sync.dma_start(x_table[:].bitcast(I32), x_words[0].rearrange("p n t -> p (n t)").bitcast(I32))
+        for r in range(4):
+            nc.sync.dma_start(es_table[r:P:32, :].bitcast(I32), es_rows[r].bitcast(I32))
+        nc.sync.dma_start(e_table[:].bitcast(I32), e_words[0].rearrange("p n t -> p (n t)").bitcast(I32))
+
+        w_bf = keep.tile([P, PACK, P, PACK], BF16, name="w_bf", tag="t4", align_bytes=64)
+        for u in range(2):
+            nc.scalar.copy(
+                out=w_bf[:].rearrange("p t m j -> p m t j")[:, u * 64 : (u + 1) * 64],
+                in_=w_raw[u][:].rearrange("p j (m t) -> p m t j", t=PACK),
+            )
+
+        xs = keep.tile([P, S], U8, name="xs", align_bytes=64)
+        nc.vector.tensor_copy(xs[:], xs_table[:].indirect(offs_sb[:]))
+        half_row = keep.tile([P, U], F32, name="half_row", tag="t1", align_bytes=64)
+        nc.vector.tensor_copy(half_row[:], half_table[:].indirect(pro_sb[:]))
+
+        w_codes = keep.tile([P, H], U32, name="w_codes", tag="t2", align_bytes=64)
+        w_scales = keep.tile([P, H], U8, name="w_scales", align_bytes=64)
+        nc.vector.quantize_mx(
+            out=w_codes[:].bitcast(FP8X4), scales=w_scales[:], in_=w_bf[:].rearrange("p t m j -> p (t m j)")
+        )
+        xc = keep.tile([P, S], U32, name="xc", tag="t4", align_bytes=64)
+        for g in range(2):
+            nc.vector.tensor_copy(xc[:, g * HALF : (g + 1) * HALF], x_table[:].indirect(offs_sb[:, g * 16 : (g + 1) * 16]))
+
+        es = tables.tile([P, U], U8, name="es", offset=0, align_bytes=64)
+        nc.vector.tensor_copy(es[:], es_table[:].indirect(pro_sb[:]))
+
+        prior_t = psum.tile([P, V], F32, name="prior_t", tag="y2")
+        nc.tensor.transpose(prior_t[:], prior_sb[:], ident[:])
+        neg_prior = keep.tile([P, 1], F32, name="neg_prior")
+        nc.scalar.activation(out=neg_prior[:], in_=prior_t[:, 0:1], func=ACT.Copy, scale=-1.0)
+        half_t = psum.tile([P, D, P], F32, name="half_t", tag="y3")
+        for d in range(D):
+            nc.tensor.transpose(half_t[:, d, :], half_row[:, d:U:D], ident[:])
+        c_col = keep.tile([P, D], F32, name="c_col")
+        nc.scalar.activation(out=c_col[:], in_=half_t[:, :, 0], func=ACT.Identity, bias=neg_prior[:], scale=1.0)
+        c_ps = psum.tile([P, D, V], F32, name="c_ps", tag="y1")
+        for d in range(D):
+            nc.tensor.transpose(c_ps[:, d, :], c_col[:, d : d + 1].to_broadcast([P, P]), ident[:])
+        c_sb = keep.tile([P, D, V], F32, name="c_sb")
+        nc.scalar.copy(out=c_sb[:], in_=c_ps[:])
+
+        h_bfs, h_codes, h_scales = [], [], []
+        for b in range(S // P):
+            cols = slice(b * P, (b + 1) * P)
+            h_ps = psum.tile([P, PACK, P], F32, name=f"h_ps{b}", tag=f"h{b}")
+            for t in range(PACK):
+                wc = slice(t * P, (t + 1) * P)
+                nc.tensor.matmul_mx(
+                    out=h_ps[:, t, :],
+                    lhsT=w_codes[:, wc].bitcast(FP8X4),
+                    lhsT_scale=w_scales[:, wc],
+                    rhs=xc[:, cols].bitcast(FP8X4),
+                    rhs_scale=xs[:, cols],
+                    start=True,
+                    stop=True,
+                )
+            h_bf = keep.tile([P, P, PACK], BF16, name=f"h_bf{b}", tag=f"hb{b}", align_bytes=64)
+            nc.scalar.copy(out=h_bf[:], in_=h_ps[:].rearrange("p t n -> p n t"))
+            h_bfs.append(h_bf)
+
+        def quantise_h(b, hc):
+            hs = keep.tile([P, P], U8, name=f"h_scales{b}", align_bytes=64)
+            nc.vector.quantize_mx(out=hc[:].bitcast(FP8X4), scales=hs[:], in_=h_bfs[b][:].rearrange("p n t -> p (n t)"))
+            h_codes.append(hc)
+            h_scales.append(hs)
+
+        quantise_h(0, keep.tile([P, P], U32, name="h_codes0", tag="t3", align_bytes=64))
+
+        ec = keep.tile([P, U], U32, name="ec", tag="hb0", align_bytes=64)
+        for g in range(2):
+            nc.vector.tensor_copy(ec[:, g * HALF : (g + 1) * HALF], e_table[:].indirect(pro_sb[:, g * 16 : (g + 1) * 16]))
+
+        nb = S // P
+        for b in range(1, nb):
+            quantise_h(b, tables.tile([P, P], U32, name=f"h_codes{b}", offset=4 * TABLE + 512 * b, align_bytes=64))
+        z = [keep.tile([P, U], F32, name=f"z{b}") for b in range(nb)]
+        low = [keep.tile([P, 1], F32, name=f"low{b}") for b in range(nb)]
+        ee = [keep.tile([P, U], F32, name=f"ee{b}") for b in range(nb)]
+        total = [keep.tile([P, 2], F32, name="total0")] + [keep.tile([P, 1], F32, name=f"total{b}") for b in range(1, nb)]
+
+        def product(b):
+            y_ps = psum.tile([P, U], F32, name=f"y_ps{b}", tag=f"y{b}")
+            width = HALF if b == 0 else U
+            for n0 in range(0, U, width):
+                cols = slice(n0, n0 + width)
+                nc.tensor.matmul_mx(
+                    out=y_ps[:, cols],
+                    lhsT=h_codes[b][:].bitcast(FP8X4),
+                    lhsT_scale=h_scales[b][:],
+                    rhs=ec[:, cols].bitcast(FP8X4),
+                    rhs_scale=es[:, cols],
+                    start=True,
+                    stop=True,
+                )
+            nc.vector.tensor_tensor(
+                out=z[b][:].rearrange("p (d v) -> p d v", d=D),
+                in0=c_sb[:],
+                in1=y_ps[:].rearrange("p (v d) -> p d v", d=D),
+                op=ALU.subtract,
+            )
+
+        def exponentiate(b):
+            nc.vector.tensor_reduce(out=low[b][:], in_=z[b][:], axis=AX.X, op=ALU.min)
+            nc.scalar.activation(
+                out=ee[b][:], in_=z[b][:], func=ACT.Exp, bias=low[b][:], scale=-1.0, accum_out=(total[0][:, b : b + 1] if b < 2 else total[b][:])
+            )
+
+        inv = [keep.tile([P, 2], F32, name=f"inv{b}") for b in range(2)]
+        for b0 in range(0, nb, 2):
+            for b in (b0, b0 + 1):
+                product(b)
+            if b0 > 0:
+                nc.vector.reciprocal(out=inv[0][:], in_=total[0][:])
+            for b in (b0, b0 + 1):
+                exponentiate(b)
+
+        res = [keep.tile([P, V], F32, name=f"res{b}") for b in range(nb)]
+        for b in range(ON_TENSOR):
+            sum_t = psum.tile([P, P], F32, name=f"sum_t{b}", tag=f"h{b}")
+            for d in range(D):
+                nc.tensor.matmul(
+                    out=sum_t[:], lhsT=ee[b][:, d * V : (d + 1) * V], rhs=ident[:],
+                    is_transpose=True, start=(d == 0), stop=(d == D - 1),
+                )
+            sum_sb = keep.tile([P, P], F32, name=f"sum_sb{b}")
+            nc.scalar.copy(out=sum_sb[:], in_=sum_t[:])
+            back = psum.tile([P, V], F32, name=f"back{b}", tag=f"y{b}")
+            nc.tensor.transpose(back[:], sum_sb[:], ident[:])
+            nc.scalar.activation(out=res[b][:], in_=back[:], func=ACT.Copy, scale=inv[0][:, b : b + 1])
+            nc.sync.dma_start(out[b * P : (b + 1) * P, :], res[b][:])
+        for b in range(ON_TENSOR, nb):
+            pairs = keep.tile([P, 2 * V], F32, name=f"pairs{b}")
+            sums = keep.tile([P, V], F32, name=f"sums{b}")
+            nc.vector.tensor_tensor(out=pairs[:], in0=ee[b][:, : 2 * V], in1=ee[b][:, 2 * V :], op=ALU.add)
+            nc.vector.reciprocal(out=inv[1][:, b - 2 : b - 1], in_=total[b][:])
+            nc.vector.tensor_tensor(out=sums[:], in0=pairs[:, :V], in1=pairs[:, V:], op=ALU.add)
+            nc.vector.tensor_scalar(out=res[b][:], in0=sums[:], scalar1=inv[1][:, b - 2 : b - 1], scalar2=None, op0=ALU.mult)
+            nc.sync.dma_start(out[b * P : (b + 1) * P, :], res[b][:])

@@ -21,9 +21,14 @@ H = 512
 U = 512
 D = 4
 V = 128
+BLOCKS = S // P
+LIST_ROWS = 16
+QUADRANT = 32
+SCALE_ROWS = 4
 HALF = 256
-ON_TENSOR = 2
-FLOPS = 2 * 512 * 512 * 512 * 2
+WORDS_BYTES = 4 * TABLE
+PAIR = 2
+FLOPS = 2 * 512 * H * S + 2 * H * S * U
 
 
 def tile_picked_yparz_post_p_kernel(
@@ -35,14 +40,14 @@ def tile_picked_yparz_post_p_kernel(
         tables = ctx.enter_context(tc.tile_pool(name="tables", bufs=1))
         psum = ctx.enter_context(tc.psum_pool(name="psum", bufs=1))
 
-        offs_sb = keep.tile([P, S // 16], U16, name="offs_sb")
-        pro_sb = keep.tile([P, U // 16], U16, name="pro_sb")
-        xs_table = keep.tile([P, TABLE], U8, name="xs_table", tag="t1", align_bytes=64)
-        es_table = keep.tile([P, TABLE], U8, name="es_table", tag="t3", align_bytes=64)
-        half_table = keep.tile([P, TABLE], F32, name="half_table", tag="t2", align_bytes=64)
-        zeros = tables.tile([P, P], F32, name="zeros", offset=4 * TABLE - 256, align_bytes=64)
+        offs_sb = keep.tile([P, S // LIST_ROWS], U16, name="offs_sb")
+        pro_sb = keep.tile([P, U // LIST_ROWS], U16, name="pro_sb")
+        xs_table = keep.tile([P, TABLE], U8, name="xs_table", tag="xs_then_half", align_bytes=64)
+        es_table = keep.tile([P, TABLE], U8, name="es_table", tag="es_then_h0", align_bytes=64)
+        half_table = keep.tile([P, TABLE], F32, name="half_table", tag="half_then_w", align_bytes=64)
+        zeros = tables.tile([P, P], F32, name="zeros", offset=WORDS_BYTES - 2 * P, align_bytes=64)
         x_table = tables.tile([P, TABLE], U32, name="x_table", offset=0, align_bytes=64)
-        e_table = tables.tile([P, TABLE], U32, name="e_table", offset=4 * TABLE, align_bytes=64)
+        e_table = tables.tile([P, TABLE], U32, name="e_table", offset=WORDS_BYTES, align_bytes=64)
         prior_sb = keep.tile([P, V], F32, name="prior_sb")
         w_raw = [keep.tile([P, PACK, HALF], F32, name=f"w_raw{u}") for u in range(2)]
 
@@ -57,40 +62,43 @@ def tile_picked_yparz_post_p_kernel(
         nc.gpsimd.dma_start(prior_sb[:], prior)
 
         w_rows = w1.rearrange("(p j) c -> p j c", j=PACK)
-        xs_rows = x_scales[0].rearrange("(q r) c -> r q c", r=4)
-        es_rows = e_scales[0].rearrange("(q r) c -> r q c", r=4)
+        xs_rows = x_scales[0].rearrange("(q r) c -> r q c", r=SCALE_ROWS)
+        es_rows = e_scales[0].rearrange("(q r) c -> r q c", r=SCALE_ROWS)
         nc.sync.dma_start(offs_sb[:], offs)
         nc.sync.dma_start(pro_sb[:], pro)
-        for r in range(4):
-            nc.sync.dma_start(xs_table[r:P:32, :].bitcast(I32), xs_rows[r].bitcast(I32))
+        for r in range(SCALE_ROWS):
+            nc.sync.dma_start(xs_table[r:P:QUADRANT, :].bitcast(I32), xs_rows[r].bitcast(I32))
         nc.sync.dma_start(w_raw[0][:], w_rows[:, :, :HALF])
         nc.sync.dma_start(w_raw[1][:], w_rows[:, :, HALF:])
         nc.sync.dma_start(half_table[0:1, :], half[0:1, :])
         nc.sync.dma_start(x_table[:].bitcast(I32), x_words[0].rearrange("p n t -> p (n t)").bitcast(I32))
-        for r in range(4):
-            nc.sync.dma_start(es_table[r:P:32, :].bitcast(I32), es_rows[r].bitcast(I32))
+        for r in range(SCALE_ROWS):
+            nc.sync.dma_start(es_table[r:P:QUADRANT, :].bitcast(I32), es_rows[r].bitcast(I32))
         nc.sync.dma_start(e_table[:].bitcast(I32), e_words[0].rearrange("p n t -> p (n t)").bitcast(I32))
 
-        w_bf = keep.tile([P, PACK, P, PACK], BF16, name="w_bf", tag="t4", align_bytes=64)
+        w_bf = keep.tile([P, PACK, P, PACK], BF16, name="w_bf", tag="w_then_x", align_bytes=64)
         for u in range(2):
             nc.scalar.copy(
-                out=w_bf[:].rearrange("p t m j -> p m t j")[:, u * 64 : (u + 1) * 64],
+                out=w_bf[:].rearrange("p t m j -> p m t j")[:, u * HALF // PACK : (u + 1) * HALF // PACK],
                 in_=w_raw[u][:].rearrange("p j (m t) -> p m t j", t=PACK),
             )
 
+        def half_list(list_sb, g):
+            return list_sb[:, g * HALF // LIST_ROWS : (g + 1) * HALF // LIST_ROWS]
+
         xs = keep.tile([P, S], U8, name="xs", align_bytes=64)
         nc.vector.tensor_copy(xs[:], xs_table[:].indirect(offs_sb[:]))
-        half_row = keep.tile([P, U], F32, name="half_row", tag="t1", align_bytes=64)
+        half_row = keep.tile([P, U], F32, name="half_row", tag="xs_then_half", align_bytes=64)
         nc.vector.tensor_copy(half_row[:], half_table[:].indirect(pro_sb[:]))
 
-        w_codes = keep.tile([P, H], U32, name="w_codes", tag="t2", align_bytes=64)
+        w_codes = keep.tile([P, H], U32, name="w_codes", tag="half_then_w", align_bytes=64)
         w_scales = keep.tile([P, H], U8, name="w_scales", align_bytes=64)
         nc.vector.quantize_mx(
             out=w_codes[:].bitcast(FP8X4), scales=w_scales[:], in_=w_bf[:].rearrange("p t m j -> p (t m j)")
         )
-        xc = keep.tile([P, S], U32, name="xc", tag="t4", align_bytes=64)
+        xc = keep.tile([P, S], U32, name="xc", tag="w_then_x", align_bytes=64)
         for g in range(2):
-            nc.vector.tensor_copy(xc[:, g * HALF : (g + 1) * HALF], x_table[:].indirect(offs_sb[:, g * 16 : (g + 1) * 16]))
+            nc.vector.tensor_copy(xc[:, g * HALF : (g + 1) * HALF], x_table[:].indirect(half_list(offs_sb, g)))
 
         es = tables.tile([P, U], U8, name="es", offset=0, align_bytes=64)
         nc.vector.tensor_copy(es[:], es_table[:].indirect(pro_sb[:]))
@@ -111,17 +119,17 @@ def tile_picked_yparz_post_p_kernel(
         nc.scalar.copy(out=c_sb[:], in_=c_ps[:])
 
         h_bfs, h_codes, h_scales = [], [], []
-        for b in range(S // P):
-            cols = slice(b * P, (b + 1) * P)
+        for b in range(BLOCKS):
+            samples = slice(b * P, (b + 1) * P)
             h_ps = psum.tile([P, PACK, P], F32, name=f"h_ps{b}", tag=f"h{b}")
             for t in range(PACK):
-                wc = slice(t * P, (t + 1) * P)
+                channels = slice(t * P, (t + 1) * P)
                 nc.tensor.matmul_mx(
                     out=h_ps[:, t, :],
-                    lhsT=w_codes[:, wc].bitcast(FP8X4),
-                    lhsT_scale=w_scales[:, wc],
-                    rhs=xc[:, cols].bitcast(FP8X4),
-                    rhs_scale=xs[:, cols],
+                    lhsT=w_codes[:, channels].bitcast(FP8X4),
+                    lhsT_scale=w_scales[:, channels],
+                    rhs=xc[:, samples].bitcast(FP8X4),
+                    rhs_scale=xs[:, samples],
                     start=True,
                     stop=True,
                 )
@@ -129,64 +137,70 @@ def tile_picked_yparz_post_p_kernel(
             nc.scalar.copy(out=h_bf[:], in_=h_ps[:].rearrange("p t n -> p n t"))
             h_bfs.append(h_bf)
 
-        def quantise_h(b, hc):
-            hs = keep.tile([P, P], U8, name=f"h_scales{b}", align_bytes=64)
-            nc.vector.quantize_mx(out=hc[:].bitcast(FP8X4), scales=hs[:], in_=h_bfs[b][:].rearrange("p n t -> p (n t)"))
-            h_codes.append(hc)
-            h_scales.append(hs)
+        def quantise_h(b, codes):
+            scales = keep.tile([P, P], U8, name=f"h_scales{b}", align_bytes=64)
+            nc.vector.quantize_mx(
+                out=codes[:].bitcast(FP8X4), scales=scales[:], in_=h_bfs[b][:].rearrange("p n t -> p (n t)")
+            )
+            h_codes.append(codes)
+            h_scales.append(scales)
 
-        quantise_h(0, keep.tile([P, P], U32, name="h_codes0", tag="t3", align_bytes=64))
+        quantise_h(0, keep.tile([P, P], U32, name="h_codes0", tag="es_then_h0", align_bytes=64))
 
         ec = keep.tile([P, U], U32, name="ec", tag="hb0", align_bytes=64)
         for g in range(2):
-            nc.vector.tensor_copy(ec[:, g * HALF : (g + 1) * HALF], e_table[:].indirect(pro_sb[:, g * 16 : (g + 1) * 16]))
+            nc.vector.tensor_copy(ec[:, g * HALF : (g + 1) * HALF], e_table[:].indirect(half_list(pro_sb, g)))
 
-        nb = S // P
-        for b in range(1, nb):
-            quantise_h(b, tables.tile([P, P], U32, name=f"h_codes{b}", offset=4 * TABLE + 512 * b, align_bytes=64))
-        z = [keep.tile([P, U], F32, name=f"z{b}") for b in range(nb)]
-        low = [keep.tile([P, 1], F32, name=f"low{b}") for b in range(nb)]
-        ee = [keep.tile([P, U], F32, name=f"ee{b}") for b in range(nb)]
-        total = [keep.tile([P, 2], F32, name="total0")] + [keep.tile([P, 1], F32, name=f"total{b}") for b in range(1, nb)]
+        for b in range(1, BLOCKS):
+            quantise_h(b, tables.tile([P, P], U32, name=f"h_codes{b}", offset=WORDS_BYTES + 4 * P * b, align_bytes=64))
+
+        cost = [keep.tile([P, U], F32, name=f"cost{b}") for b in range(BLOCKS)]
+        low = [keep.tile([P, 1], F32, name=f"low{b}") for b in range(BLOCKS)]
+        ee = [keep.tile([P, U], F32, name=f"ee{b}") for b in range(BLOCKS)]
+        first_totals = keep.tile([P, PAIR], F32, name="first_totals")
+        total = [first_totals[:, b : b + 1] for b in range(PAIR)]
+        total += [keep.tile([P, 1], F32, name=f"total{b}")[:] for b in range(PAIR, BLOCKS)]
 
         def product(b):
             y_ps = psum.tile([P, U], F32, name=f"y_ps{b}", tag=f"y{b}")
             width = HALF if b == 0 else U
             for n0 in range(0, U, width):
-                cols = slice(n0, n0 + width)
+                protos = slice(n0, n0 + width)
                 nc.tensor.matmul_mx(
-                    out=y_ps[:, cols],
+                    out=y_ps[:, protos],
                     lhsT=h_codes[b][:].bitcast(FP8X4),
                     lhsT_scale=h_scales[b][:],
-                    rhs=ec[:, cols].bitcast(FP8X4),
-                    rhs_scale=es[:, cols],
+                    rhs=ec[:, protos].bitcast(FP8X4),
+                    rhs_scale=es[:, protos],
                     start=True,
                     stop=True,
                 )
             nc.vector.tensor_tensor(
-                out=z[b][:].rearrange("p (d v) -> p d v", d=D),
+                out=cost[b][:].rearrange("p (d v) -> p d v", d=D),
                 in0=c_sb[:],
                 in1=y_ps[:].rearrange("p (v d) -> p d v", d=D),
                 op=ALU.subtract,
             )
 
         def exponentiate(b):
-            nc.vector.tensor_reduce(out=low[b][:], in_=z[b][:], axis=AX.X, op=ALU.min)
+            nc.vector.tensor_reduce(out=low[b][:], in_=cost[b][:], axis=AX.X, op=ALU.min)
             nc.scalar.activation(
-                out=ee[b][:], in_=z[b][:], func=ACT.Exp, bias=low[b][:], scale=-1.0, accum_out=(total[0][:, b : b + 1] if b < 2 else total[b][:])
+                out=ee[b][:], in_=cost[b][:], func=ACT.Exp, bias=low[b][:], scale=-1.0, accum_out=total[b]
             )
 
-        inv = [keep.tile([P, 2], F32, name=f"inv{b}") for b in range(2)]
-        for b0 in range(0, nb, 2):
-            for b in (b0, b0 + 1):
-                product(b)
-            if b0 > 0:
-                nc.vector.reciprocal(out=inv[0][:], in_=total[0][:])
-            for b in (b0, b0 + 1):
-                exponentiate(b)
+        inv = [keep.tile([P, PAIR], F32, name=f"inv{pair}") for pair in range(BLOCKS // PAIR)]
+        for b in range(PAIR):
+            product(b)
+        for b in range(PAIR):
+            exponentiate(b)
+        for b in range(PAIR, BLOCKS):
+            product(b)
+        nc.vector.reciprocal(out=inv[0][:], in_=first_totals[:])
+        for b in range(PAIR, BLOCKS):
+            exponentiate(b)
 
-        res = [keep.tile([P, V], F32, name=f"res{b}") for b in range(nb)]
-        for b in range(ON_TENSOR):
+        res = [keep.tile([P, V], F32, name=f"res{b}") for b in range(BLOCKS)]
+        for b in range(PAIR):
             sum_t = psum.tile([P, P], F32, name=f"sum_t{b}", tag=f"h{b}")
             for d in range(D):
                 nc.tensor.matmul(
@@ -199,11 +213,12 @@ def tile_picked_yparz_post_p_kernel(
             nc.tensor.transpose(back[:], sum_sb[:], ident[:])
             nc.scalar.activation(out=res[b][:], in_=back[:], func=ACT.Copy, scale=inv[0][:, b : b + 1])
             nc.sync.dma_start(out[b * P : (b + 1) * P, :], res[b][:])
-        for b in range(ON_TENSOR, nb):
-            pairs = keep.tile([P, 2 * V], F32, name=f"pairs{b}")
+        for b in range(PAIR, BLOCKS):
+            halves = keep.tile([P, 2 * V], F32, name=f"halves{b}")
             sums = keep.tile([P, V], F32, name=f"sums{b}")
-            nc.vector.tensor_tensor(out=pairs[:], in0=ee[b][:, : 2 * V], in1=ee[b][:, 2 * V :], op=ALU.add)
-            nc.vector.reciprocal(out=inv[1][:, b - 2 : b - 1], in_=total[b][:])
-            nc.vector.tensor_tensor(out=sums[:], in0=pairs[:, :V], in1=pairs[:, V:], op=ALU.add)
-            nc.vector.tensor_scalar(out=res[b][:], in0=sums[:], scalar1=inv[1][:, b - 2 : b - 1], scalar2=None, op0=ALU.mult)
+            inv_b = inv[1][:, b - PAIR : b - PAIR + 1]
+            nc.vector.tensor_tensor(out=halves[:], in0=ee[b][:, : 2 * V], in1=ee[b][:, 2 * V :], op=ALU.add)
+            nc.vector.reciprocal(out=inv_b, in_=total[b])
+            nc.vector.tensor_tensor(out=sums[:], in0=halves[:, :V], in1=halves[:, V:], op=ALU.add)
+            nc.vector.tensor_scalar(out=res[b][:], in0=sums[:], scalar1=inv_b, scalar2=None, op0=ALU.mult)
             nc.sync.dma_start(out[b * P : (b + 1) * P, :], res[b][:])

@@ -1,6 +1,7 @@
 from contextlib import ExitStack
 
 import concourse.mybir as mybir
+from concourse.masks import make_identity
 
 F32 = mybir.dt.float32
 BF16 = mybir.dt.bfloat16
@@ -22,12 +23,12 @@ U = 512
 D = 4
 V = 128
 BLOCKS = S // P
+TILES = U // P
 LIST_ROWS = 16
 QUADRANT = 32
 SCALE_ROWS = 4
 HALF = 256
 WORDS_BYTES = 4 * TABLE
-PAIR = 2
 FLOPS = 2 * 512 * H * S + 2 * H * S * U
 
 
@@ -45,43 +46,46 @@ def tile_picked_yparz_post_p_kernel(
         xs_table = keep.tile([P, TABLE], U8, name="xs_table", tag="xs_then_half", align_bytes=64)
         es_table = keep.tile([P, TABLE], U8, name="es_table", tag="es_then_h0", align_bytes=64)
         half_table = keep.tile([P, TABLE], F32, name="half_table", tag="half_then_w", align_bytes=64)
-        zeros = tables.tile([P, P], F32, name="zeros", offset=WORDS_BYTES - 2 * P, align_bytes=64)
         x_table = tables.tile([P, TABLE], U32, name="x_table", offset=0, align_bytes=64)
         e_table = tables.tile([P, TABLE], U32, name="e_table", offset=WORDS_BYTES, align_bytes=64)
-        prior_sb = keep.tile([P, V], F32, name="prior_sb")
         w_raw = [keep.tile([P, PACK, HALF], F32, name=f"w_raw{u}") for u in range(2)]
+        prior_sb = keep.tile([P, V], F32, name="prior_sb")
 
         nc.vector.memset(xs_table[:].bitcast(I32), 0)
-        nc.vector.memset(es_table[:].bitcast(I32), 0)
         nc.vector.memset(half_table[:], 0.0)
-        nc.vector.memset(zeros[:], 0.0)
-        ident = keep.tile([P, P], F32, name="ident")
-        nc.gpsimd.affine_select(
-            out=ident[:], in_=zeros[:], compare_op=ALU.not_equal, fill=1.0, base=0, pattern=[[-1, P]], channel_multiplier=1
-        )
+        nc.vector.memset(es_table[:].bitcast(I32), 0)
         nc.gpsimd.dma_start(prior_sb[:], prior)
+        ident = keep.tile([P, P], F32, name="ident")
+        make_identity(nc, ident[:])
 
         w_rows = w1.rearrange("(p j) c -> p j c", j=PACK)
         xs_rows = x_scales[0].rearrange("(q r) c -> r q c", r=SCALE_ROWS)
         es_rows = e_scales[0].rearrange("(q r) c -> r q c", r=SCALE_ROWS)
         nc.sync.dma_start(offs_sb[:], offs)
         nc.sync.dma_start(pro_sb[:], pro)
+        nc.sync.dma_start(w_raw[0][:], w_rows[:, :, :HALF])
         for r in range(SCALE_ROWS):
             nc.sync.dma_start(xs_table[r:P:QUADRANT, :].bitcast(I32), xs_rows[r].bitcast(I32))
-        nc.sync.dma_start(w_raw[0][:], w_rows[:, :, :HALF])
         nc.sync.dma_start(w_raw[1][:], w_rows[:, :, HALF:])
         nc.sync.dma_start(half_table[0:1, :], half[0:1, :])
         nc.sync.dma_start(x_table[:].bitcast(I32), x_words[0].rearrange("p n t -> p (n t)").bitcast(I32))
         for r in range(SCALE_ROWS):
             nc.sync.dma_start(es_table[r:P:QUADRANT, :].bitcast(I32), es_rows[r].bitcast(I32))
-        nc.sync.dma_start(e_table[:].bitcast(I32), e_words[0].rearrange("p n t -> p (n t)").bitcast(I32))
 
         w_bf = keep.tile([P, PACK, P, PACK], BF16, name="w_bf", tag="w_then_x", align_bytes=64)
         for u in range(2):
-            nc.scalar.copy(
+            nc.scalar.activation(
                 out=w_bf[:].rearrange("p t m j -> p m t j")[:, u * HALF // PACK : (u + 1) * HALF // PACK],
                 in_=w_raw[u][:].rearrange("p j (m t) -> p m t j", t=PACK),
+                func=ACT.Copy,
             )
+        nc.sync.dma_start(e_table[:].bitcast(I32), e_words[0].rearrange("p n t -> p (n t)").bitcast(I32))
+
+        neg_prior = keep.tile([P, V, D], F32, name="neg_prior")
+        nc.gpsimd.tensor_scalar(
+            out=neg_prior[:], in0=prior_sb[:].unsqueeze(2).to_broadcast([P, V, D]), scalar1=-1.0, scalar2=0.0,
+            op0=ALU.mult, op1=ALU.add,
+        )
 
         def half_list(list_sb, g):
             return list_sb[:, g * HALF // LIST_ROWS : (g + 1) * HALF // LIST_ROWS]
@@ -103,22 +107,16 @@ def tile_picked_yparz_post_p_kernel(
         es = tables.tile([P, U], U8, name="es", offset=0, align_bytes=64)
         nc.vector.tensor_copy(es[:], es_table[:].indirect(pro_sb[:]))
 
-        prior_t = psum.tile([P, V], F32, name="prior_t", tag="y2")
-        nc.tensor.transpose(prior_t[:], prior_sb[:], ident[:])
-        neg_prior = keep.tile([P, 1], F32, name="neg_prior")
-        nc.scalar.activation(out=neg_prior[:], in_=prior_t[:, 0:1], func=ACT.Copy, scale=-1.0)
-        half_t = psum.tile([P, D, P], F32, name="half_t", tag="y3")
-        for d in range(D):
-            nc.tensor.transpose(half_t[:, d, :], half_row[:, d:U:D], ident[:])
-        c_col = keep.tile([P, D], F32, name="c_col")
-        nc.scalar.activation(out=c_col[:], in_=half_t[:, :, 0], func=ACT.Identity, bias=neg_prior[:], scale=1.0)
-        c_ps = psum.tile([P, D, V], F32, name="c_ps", tag="y1")
-        for d in range(D):
-            nc.tensor.transpose(c_ps[:, d, :], c_col[:, d : d + 1].to_broadcast([P, P]), ident[:])
-        c_sb = keep.tile([P, D, V], F32, name="c_sb")
-        nc.scalar.copy(out=c_sb[:], in_=c_ps[:])
+        c_ps = psum.tile([P, TILES, P], F32, name="c_ps", tag="y11")
+        neg_flat = neg_prior[:].rearrange("p v d -> p (v d)")
+        for jb in range(TILES):
+            protos = slice(jb * P, (jb + 1) * P)
+            nc.tensor.matmul(out=c_ps[:, jb, :], lhsT=neg_flat[:, protos], rhs=ident[:], is_transpose=True, start=True, stop=False)
+            nc.tensor.matmul(out=c_ps[:, jb, :], lhsT=half_row[:, protos], rhs=ident[:], is_transpose=True, start=False, stop=True)
+        c_col = keep.tile([P, TILES], F32, name="c_col")
+        nc.scalar.copy(out=c_col[:], in_=c_ps[:, :, 0])
 
-        h_bfs, h_codes, h_scales = [], [], []
+        h_bfs = []
         for b in range(BLOCKS):
             samples = slice(b * P, (b + 1) * P)
             h_ps = psum.tile([P, PACK, P], F32, name=f"h_ps{b}", tag=f"h{b}")
@@ -137,88 +135,72 @@ def tile_picked_yparz_post_p_kernel(
             nc.scalar.copy(out=h_bf[:], in_=h_ps[:].rearrange("p t n -> p n t"))
             h_bfs.append(h_bf)
 
-        def quantise_h(b, codes):
-            scales = keep.tile([P, P], U8, name=f"h_scales{b}", align_bytes=64)
-            nc.vector.quantize_mx(
-                out=codes[:].bitcast(FP8X4), scales=scales[:], in_=h_bfs[b][:].rearrange("p n t -> p (n t)")
-            )
-            h_codes.append(codes)
-            h_scales.append(scales)
+        h_scales = [keep.tile([P, HALF], U8, name=f"h_scales{g}", align_bytes=64) for g in range(2)]
 
-        quantise_h(0, keep.tile([P, P], U32, name="h_codes0", tag="es_then_h0", align_bytes=64))
+        def quantise_h(codes, g):
+            for u in range(2):
+                nc.vector.quantize_mx(
+                    out=codes[:, u * P : (u + 1) * P].bitcast(FP8X4),
+                    scales=h_scales[g][:, u * P : (u + 1) * P],
+                    in_=h_bfs[2 * g + u][:].rearrange("p n t -> p (n t)"),
+                )
 
-        ec = keep.tile([P, U], U32, name="ec", tag="hb0", align_bytes=64)
+        h_codes = [keep.tile([P, HALF], U32, name="h_codes0", tag="es_then_h0", align_bytes=64)]
+        quantise_h(h_codes[0], 0)
+        ec = keep.tile([P, U], U32, name="ec", tag="hb1", align_bytes=64)
         for g in range(2):
             nc.vector.tensor_copy(ec[:, g * HALF : (g + 1) * HALF], e_table[:].indirect(half_list(pro_sb, g)))
+        h_codes.append(tables.tile([P, HALF], U32, name="h_codes1", offset=WORDS_BYTES, align_bytes=64))
+        quantise_h(h_codes[1], 1)
 
-        for b in range(1, BLOCKS):
-            quantise_h(b, tables.tile([P, P], U32, name=f"h_codes{b}", offset=WORDS_BYTES + 4 * P * b, align_bytes=64))
+        cost_t = [[keep.tile([P, HALF], F32, name=f"cost_t{g}{jb}") for jb in range(TILES)] for g in range(2)]
+        for g in range(2):
+            for pair in range(TILES // 2):
+                y_ps = psum.tile([P, 2, HALF], F32, name=f"y_ps{g}{pair}", tag=f"y{g}{pair}")
+                for u in range(2):
+                    protos = slice((2 * pair + u) * P, (2 * pair + u + 1) * P)
+                    nc.tensor.matmul_mx(
+                        out=y_ps[:, u, :],
+                        lhsT=ec[:, protos].bitcast(FP8X4),
+                        lhsT_scale=es[:, protos],
+                        rhs=h_codes[g][:].bitcast(FP8X4),
+                        rhs_scale=h_scales[g][:],
+                        start=True,
+                        stop=True,
+                    )
+                for u in range(2):
+                    jb = 2 * pair + u
+                    if (g, pair) == (1, 0):
+                        nc.vector.tensor_scalar(
+                            out=cost_t[g][jb][:], in0=y_ps[:, u, :], scalar1=-1.0, scalar2=c_col[:, jb : jb + 1],
+                            op0=ALU.mult, op1=ALU.add,
+                        )
+                    else:
+                        nc.scalar.activation(
+                            out=cost_t[g][jb][:], in_=y_ps[:, u, :], func=ACT.Identity, bias=c_col[:, jb : jb + 1], scale=-1.0
+                        )
 
-        cost = [keep.tile([P, U], F32, name=f"cost{b}") for b in range(BLOCKS)]
         low = [keep.tile([P, 1], F32, name=f"low{b}") for b in range(BLOCKS)]
-        ee = [keep.tile([P, U], F32, name=f"ee{b}") for b in range(BLOCKS)]
-        first_totals = keep.tile([P, PAIR], F32, name="first_totals")
-        total = [first_totals[:, b : b + 1] for b in range(PAIR)]
-        total += [keep.tile([P, 1], F32, name=f"total{b}")[:] for b in range(PAIR, BLOCKS)]
-
-        def product(b):
-            y_ps = psum.tile([P, U], F32, name=f"y_ps{b}", tag=f"y{b}")
-            width = HALF if b == 0 else U
-            for n0 in range(0, U, width):
-                protos = slice(n0, n0 + width)
-                nc.tensor.matmul_mx(
-                    out=y_ps[:, protos],
-                    lhsT=h_codes[b][:].bitcast(FP8X4),
-                    lhsT_scale=h_scales[b][:],
-                    rhs=ec[:, protos].bitcast(FP8X4),
-                    rhs_scale=es[:, protos],
-                    start=True,
-                    stop=True,
-                )
-            nc.vector.tensor_tensor(
-                out=cost[b][:].rearrange("p (d v) -> p d v", d=D),
-                in0=c_sb[:],
-                in1=y_ps[:].rearrange("p (v d) -> p d v", d=D),
-                op=ALU.subtract,
-            )
-
-        def exponentiate(b):
-            nc.vector.tensor_reduce(out=low[b][:], in_=cost[b][:], axis=AX.X, op=ALU.min)
+        total = [keep.tile([P, 1], F32, name=f"total{b}") for b in range(BLOCKS)]
+        ee = [keep.tile([P, D, V], F32, name=f"ee{b}") for b in range(BLOCKS)]
+        for b in range(BLOCKS):
+            g, u = divmod(b, 2)
+            cost = psum.tile([P, U], F32, name=f"cost{b}", tag=f"h{b}")
+            for jb in range(TILES):
+                nc.tensor.transpose(cost[:, jb * P : (jb + 1) * P], cost_t[g][jb][:, u * P : (u + 1) * P], ident[:])
+            nc.vector.tensor_reduce(out=low[b][:], in_=cost[:], axis=AX.X, op=ALU.min)
             nc.scalar.activation(
-                out=ee[b][:], in_=cost[b][:], func=ACT.Exp, bias=low[b][:], scale=-1.0, accum_out=total[b]
+                out=ee[b][:], in_=cost[:].rearrange("p (v d) -> p d v", d=D), func=ACT.Exp, bias=low[b][:], scale=-1.0,
+                accum_out=total[b][:],
             )
 
-        inv = [keep.tile([P, PAIR], F32, name=f"inv{pair}") for pair in range(BLOCKS // PAIR)]
-        for b in range(PAIR):
-            product(b)
-        for b in range(PAIR):
-            exponentiate(b)
-        for b in range(PAIR, BLOCKS):
-            product(b)
-        nc.vector.reciprocal(out=inv[0][:], in_=first_totals[:])
-        for b in range(PAIR, BLOCKS):
-            exponentiate(b)
-
-        res = [keep.tile([P, V], F32, name=f"res{b}") for b in range(BLOCKS)]
-        for b in range(PAIR):
-            sum_t = psum.tile([P, P], F32, name=f"sum_t{b}", tag=f"h{b}")
-            for d in range(D):
-                nc.tensor.matmul(
-                    out=sum_t[:], lhsT=ee[b][:, d * V : (d + 1) * V], rhs=ident[:],
-                    is_transpose=True, start=(d == 0), stop=(d == D - 1),
-                )
-            sum_sb = keep.tile([P, P], F32, name=f"sum_sb{b}")
-            nc.scalar.copy(out=sum_sb[:], in_=sum_t[:])
-            back = psum.tile([P, V], F32, name=f"back{b}", tag=f"y{b}")
-            nc.tensor.transpose(back[:], sum_sb[:], ident[:])
-            nc.scalar.activation(out=res[b][:], in_=back[:], func=ACT.Copy, scale=inv[0][:, b : b + 1])
-            nc.sync.dma_start(out[b * P : (b + 1) * P, :], res[b][:])
-        for b in range(PAIR, BLOCKS):
-            halves = keep.tile([P, 2 * V], F32, name=f"halves{b}")
+        for b in range(BLOCKS):
+            halves = keep.tile([P, 2, V], F32, name=f"halves{b}")
             sums = keep.tile([P, V], F32, name=f"sums{b}")
-            inv_b = inv[1][:, b - PAIR : b - PAIR + 1]
-            nc.vector.tensor_tensor(out=halves[:], in0=ee[b][:, : 2 * V], in1=ee[b][:, 2 * V :], op=ALU.add)
-            nc.vector.reciprocal(out=inv_b, in_=total[b])
-            nc.vector.tensor_tensor(out=sums[:], in0=halves[:, :V], in1=halves[:, V:], op=ALU.add)
-            nc.vector.tensor_scalar(out=res[b][:], in0=sums[:], scalar1=inv_b, scalar2=None, op0=ALU.mult)
-            nc.sync.dma_start(out[b * P : (b + 1) * P, :], res[b][:])
+            inv = keep.tile([P, 1], F32, name=f"inv{b}")
+            res = keep.tile([P, V], F32, name=f"res{b}")
+            nc.vector.tensor_tensor(out=halves[:], in0=ee[b][:, :2, :], in1=ee[b][:, 2:, :], op=ALU.add)
+            nc.vector.reciprocal(out=inv[:], in_=total[b][:])
+            nc.vector.tensor_tensor(out=sums[:], in0=halves[:, 0, :], in1=halves[:, 1, :], op=ALU.add)
+            nc.vector.tensor_scalar(out=res[:], in0=sums[:], scalar1=inv[:], scalar2=None, op0=ALU.mult)
+            nc.sync.dma_start(out[b * P : (b + 1) * P, :], res[:])

@@ -28,6 +28,8 @@ LIST_ROWS = 16
 QUADRANT = 32
 SCALE_ROWS = 4
 HALF = 256
+ROW_STEP = 8
+HALF_ROW = 12
 WORDS_BYTES = 4 * TABLE
 FLOPS = 2 * 512 * H * S + 2 * H * S * U
 
@@ -43,34 +45,30 @@ def tile_picked_yparz_post_p_kernel(
 
         offs_sb = keep.tile([P, S // LIST_ROWS], U16, name="offs_sb")
         pro_sb = keep.tile([P, U // LIST_ROWS], U16, name="pro_sb")
-        xs_table = keep.tile([P, TABLE], U8, name="xs_table", tag="xs_then_half", align_bytes=64)
-        es_table = keep.tile([P, TABLE], U8, name="es_table", tag="es_then_h0", align_bytes=64)
-        half_table = keep.tile([P, TABLE], F32, name="half_table", tag="half_then_w", align_bytes=64)
+        xs_table = keep.tile([P, TABLE], U8, name="xs_table", align_bytes=64)
+        es_table = keep.tile([P, TABLE], U8, name="es_table", tag="es_then_w", align_bytes=64)
+        half_table = keep.tile([P, TABLE], F32, name="half_table", tag="half_then_h", align_bytes=64)
         x_table = tables.tile([P, TABLE], U32, name="x_table", offset=0, align_bytes=64)
         e_table = tables.tile([P, TABLE], U32, name="e_table", offset=WORDS_BYTES, align_bytes=64)
         w_raw = [keep.tile([P, PACK, HALF], F32, name=f"w_raw{u}") for u in range(2)]
         prior_sb = keep.tile([P, V], F32, name="prior_sb")
 
         nc.vector.memset(xs_table[:].bitcast(I32), 0)
-        nc.vector.memset(half_table[:], 0.0)
         nc.vector.memset(es_table[:].bitcast(I32), 0)
-        nc.gpsimd.dma_start(prior_sb[:], prior)
+        nc.vector.memset(half_table[:], 0.0)
         ident = keep.tile([P, P], F32, name="ident")
         make_identity(nc, ident[:])
 
         w_rows = w1.rearrange("(p j) c -> p j c", j=PACK)
-        xs_rows = x_scales[0].rearrange("(q r) c -> r q c", r=SCALE_ROWS)
-        es_rows = e_scales[0].rearrange("(q r) c -> r q c", r=SCALE_ROWS)
         nc.sync.dma_start(offs_sb[:], offs)
-        nc.sync.dma_start(pro_sb[:], pro)
         nc.sync.dma_start(w_raw[0][:], w_rows[:, :, :HALF])
-        for r in range(SCALE_ROWS):
-            nc.sync.dma_start(xs_table[r:P:QUADRANT, :].bitcast(I32), xs_rows[r].bitcast(I32))
+        nc.sync.dma_start(pro_sb[:], pro)
+        nc.sync.dma_start(xs_table[0:P:ROW_STEP, :].bitcast(I32), x_scales[0].bitcast(I32))
+        nc.sync.dma_start(es_table[0:P:ROW_STEP, :].bitcast(I32), e_scales[0].bitcast(I32))
         nc.sync.dma_start(w_raw[1][:], w_rows[:, :, HALF:])
-        nc.sync.dma_start(half_table[0:1, :], half[0:1, :])
+        nc.sync.dma_start(prior_sb[:], prior)
         nc.sync.dma_start(x_table[:].bitcast(I32), x_words[0].rearrange("p n t -> p (n t)").bitcast(I32))
-        for r in range(SCALE_ROWS):
-            nc.sync.dma_start(es_table[r:P:QUADRANT, :].bitcast(I32), es_rows[r].bitcast(I32))
+        nc.sync.dma_start(half_table[HALF_ROW : HALF_ROW + 1, :], half[0:1, :])
 
         w_bf = keep.tile([P, PACK, P, PACK], BF16, name="w_bf", tag="w_then_x", align_bytes=64)
         for u in range(2):
@@ -79,23 +77,26 @@ def tile_picked_yparz_post_p_kernel(
                 in_=w_raw[u][:].rearrange("p j (m t) -> p m t j", t=PACK),
                 func=ACT.Copy,
             )
-        nc.sync.dma_start(e_table[:].bitcast(I32), e_words[0].rearrange("p n t -> p (n t)").bitcast(I32))
-
-        neg_prior = keep.tile([P, V, D], F32, name="neg_prior")
-        nc.gpsimd.tensor_scalar(
-            out=neg_prior[:], in0=prior_sb[:].unsqueeze(2).to_broadcast([P, V, D]), scalar1=-1.0, scalar2=0.0,
-            op0=ALU.mult, op1=ALU.add,
-        )
 
         def half_list(list_sb, g):
             return list_sb[:, g * HALF // LIST_ROWS : (g + 1) * HALF // LIST_ROWS]
 
-        xs = keep.tile([P, S], U8, name="xs", align_bytes=64)
-        nc.vector.tensor_copy(xs[:], xs_table[:].indirect(offs_sb[:]))
-        half_row = keep.tile([P, U], F32, name="half_row", tag="xs_then_half", align_bytes=64)
-        nc.vector.tensor_copy(half_row[:], half_table[:].indirect(pro_sb[:]))
+        def gather_scales(name, table, list_sb):
+            spread = keep.tile([P, S], U8, name=f"{name}_spread", align_bytes=64)
+            placed = keep.tile([P, S], U8, name=name, align_bytes=64)
+            nc.vector.tensor_copy(spread[:], table[:].indirect(list_sb[:]))
+            nc.gpsimd.memset(placed[:].bitcast(I32), 0)
+            for r in range(SCALE_ROWS):
+                nc.sync.dma_start(
+                    placed[r:P:QUADRANT, :].bitcast(I32), spread[ROW_STEP * r : P : QUADRANT, :].bitcast(I32)
+                )
+            return placed
 
-        w_codes = keep.tile([P, H], U32, name="w_codes", tag="half_then_w", align_bytes=64)
+        xs = gather_scales("xs", xs_table, offs_sb)
+        nc.sync.dma_start(e_table[:].bitcast(I32), e_words[0].rearrange("p n t -> p (n t)").bitcast(I32))
+        es = gather_scales("es", es_table, pro_sb)
+
+        w_codes = keep.tile([P, H], U32, name="w_codes", tag="es_then_w", align_bytes=64)
         w_scales = keep.tile([P, H], U8, name="w_scales", align_bytes=64)
         nc.vector.quantize_mx(
             out=w_codes[:].bitcast(FP8X4), scales=w_scales[:], in_=w_bf[:].rearrange("p t m j -> p (t m j)")
@@ -104,17 +105,13 @@ def tile_picked_yparz_post_p_kernel(
         for g in range(2):
             nc.vector.tensor_copy(xc[:, g * HALF : (g + 1) * HALF], x_table[:].indirect(half_list(offs_sb, g)))
 
-        es = tables.tile([P, U], U8, name="es", offset=0, align_bytes=64)
-        nc.vector.tensor_copy(es[:], es_table[:].indirect(pro_sb[:]))
-
-        c_ps = psum.tile([P, TILES, P], F32, name="c_ps", tag="y11")
-        neg_flat = neg_prior[:].rearrange("p v d -> p (v d)")
-        for jb in range(TILES):
-            protos = slice(jb * P, (jb + 1) * P)
-            nc.tensor.matmul(out=c_ps[:, jb, :], lhsT=neg_flat[:, protos], rhs=ident[:], is_transpose=True, start=True, stop=False)
-            nc.tensor.matmul(out=c_ps[:, jb, :], lhsT=half_row[:, protos], rhs=ident[:], is_transpose=True, start=False, stop=True)
-        c_col = keep.tile([P, TILES], F32, name="c_col")
-        nc.scalar.copy(out=c_col[:], in_=c_ps[:, :, 0])
+        prior_rep = keep.tile([P, V, D], F32, name="prior_rep")
+        nc.scalar.copy(out=prior_rep[:], in_=prior_sb[:].unsqueeze(2).to_broadcast([P, V, D]))
+        c_row = tables.tile([P, U], F32, name="c_row", offset=0, align_bytes=64)
+        nc.vector.tensor_tensor(
+            out=c_row[:], in0=half_table[:].indirect(pro_sb[:]), in1=prior_rep[:].rearrange("p v d -> p (v d)"),
+            op=ALU.subtract,
+        )
 
         h_bfs = []
         for b in range(BLOCKS):
@@ -135,6 +132,12 @@ def tile_picked_yparz_post_p_kernel(
             nc.scalar.copy(out=h_bf[:], in_=h_ps[:].rearrange("p t n -> p n t"))
             h_bfs.append(h_bf)
 
+        c_ps = psum.tile([P, TILES, P], F32, name="c_ps", tag="h0")
+        for jb in range(TILES):
+            nc.tensor.transpose(c_ps[:, jb, :], c_row[:, jb * P : (jb + 1) * P], ident[:])
+        c_col = keep.tile([P, TILES], F32, name="c_col")
+        nc.scalar.copy(out=c_col[:], in_=c_ps[:, :, HALF_ROW])
+
         h_scales = [keep.tile([P, HALF], U8, name=f"h_scales{g}", align_bytes=64) for g in range(2)]
 
         def quantise_h(codes, g):
@@ -145,7 +148,7 @@ def tile_picked_yparz_post_p_kernel(
                     in_=h_bfs[2 * g + u][:].rearrange("p n t -> p (n t)"),
                 )
 
-        h_codes = [keep.tile([P, HALF], U32, name="h_codes0", tag="es_then_h0", align_bytes=64)]
+        h_codes = [keep.tile([P, HALF], U32, name="h_codes0", tag="half_then_h", align_bytes=64)]
         quantise_h(h_codes[0], 0)
         ec = keep.tile([P, U], U32, name="ec", tag="hb1", align_bytes=64)
         for g in range(2):
@@ -170,7 +173,7 @@ def tile_picked_yparz_post_p_kernel(
                     )
                 for u in range(2):
                     jb = 2 * pair + u
-                    if (g, pair) == (1, 0):
+                    if (g, pair) == (0, 1):
                         nc.vector.tensor_scalar(
                             out=cost_t[g][jb][:], in0=y_ps[:, u, :], scalar1=-1.0, scalar2=c_col[:, jb : jb + 1],
                             op0=ALU.mult, op1=ALU.add,
@@ -181,7 +184,9 @@ def tile_picked_yparz_post_p_kernel(
                         )
 
         low = [keep.tile([P, 1], F32, name=f"low{b}") for b in range(BLOCKS)]
-        total = [keep.tile([P, 1], F32, name=f"total{b}") for b in range(BLOCKS)]
+        early_totals = keep.tile([P, BLOCKS - 1], F32, name="early_totals")
+        last_total = keep.tile([P, 1], F32, name="last_total")
+        total = [early_totals[:, b : b + 1] for b in range(BLOCKS - 1)] + [last_total[:]]
         ee = [keep.tile([P, D, V], F32, name=f"ee{b}") for b in range(BLOCKS)]
         for b in range(BLOCKS):
             g, u = divmod(b, 2)
@@ -191,16 +196,34 @@ def tile_picked_yparz_post_p_kernel(
             nc.vector.tensor_reduce(out=low[b][:], in_=cost[:], axis=AX.X, op=ALU.min)
             nc.scalar.activation(
                 out=ee[b][:], in_=cost[:].rearrange("p (v d) -> p d v", d=D), func=ACT.Exp, bias=low[b][:], scale=-1.0,
-                accum_out=total[b][:],
+                accum_out=total[b],
             )
 
+        early_inv = keep.tile([P, BLOCKS - 1], F32, name="early_inv")
+        last_inv = keep.tile([P, 1], F32, name="last_inv")
+        inv = [early_inv[:, b : b + 1] for b in range(BLOCKS - 1)] + [last_inv[:]]
+        halves = [keep.tile([P, 2, V], F32, name=f"halves{b}") for b in range(BLOCKS - 1)]
+        sums = [keep.tile([P, V], F32, name=f"sums{b}") for b in range(BLOCKS)]
+        res = [keep.tile([P, V], F32, name=f"res{b}") for b in range(BLOCKS)]
+
+        def add_pairs(b, engine):
+            engine.tensor_tensor(out=halves[b][:], in0=ee[b][:, :2, :], in1=ee[b][:, 2:, :], op=ALU.add)
+
+        def add_halves(b, engine):
+            engine.tensor_tensor(out=sums[b][:], in0=halves[b][:, 0, :], in1=halves[b][:, 1, :], op=ALU.add)
+
+        add_pairs(0, nc.gpsimd)
+        add_halves(0, nc.gpsimd)
+        add_pairs(1, nc.vector)
+        nc.vector.reciprocal(out=early_inv[:], in_=early_totals[:])
+        add_pairs(2, nc.vector)
+        add_halves(1, nc.vector)
+        add_halves(2, nc.vector)
+        nc.vector.tensor_reduce(out=sums[3][:], in_=ee[3][:].rearrange("p d v -> p v d"), axis=AX.X, op=ALU.add)
+        nc.vector.reciprocal(out=last_inv[:], in_=last_total[:])
         for b in range(BLOCKS):
-            halves = keep.tile([P, 2, V], F32, name=f"halves{b}")
-            sums = keep.tile([P, V], F32, name=f"sums{b}")
-            inv = keep.tile([P, 1], F32, name=f"inv{b}")
-            res = keep.tile([P, V], F32, name=f"res{b}")
-            nc.vector.tensor_tensor(out=halves[:], in0=ee[b][:, :2, :], in1=ee[b][:, 2:, :], op=ALU.add)
-            nc.vector.reciprocal(out=inv[:], in_=total[b][:])
-            nc.vector.tensor_tensor(out=sums[:], in0=halves[:, 0, :], in1=halves[:, 1, :], op=ALU.add)
-            nc.vector.tensor_scalar(out=res[:], in0=sums[:], scalar1=inv[:], scalar2=None, op0=ALU.mult)
-            nc.sync.dma_start(out[b * P : (b + 1) * P, :], res[:])
+            if b < BLOCKS - 1:
+                nc.scalar.activation(out=res[b][:], in_=sums[b][:], func=ACT.Copy, scale=inv[b])
+            else:
+                nc.vector.tensor_scalar(out=res[b][:], in0=sums[b][:], scalar1=inv[b], scalar2=None, op0=ALU.mult)
+            nc.sync.dma_start(out[b * P : (b + 1) * P, :], res[b][:])

@@ -60,15 +60,18 @@ def tile_picked_yparz_post_p_kernel(
         make_identity(nc, ident[:])
 
         w_rows = w1.rearrange("(p j) c -> p j c", j=PACK)
+        xs_rows = x_scales[0].rearrange("(q r) c -> r q c", r=SCALE_ROWS)
         nc.sync.dma_start(offs_sb[:], offs)
         nc.sync.dma_start(w_raw[0][:], w_rows[:, :, :HALF])
-        nc.sync.dma_start(pro_sb[:], pro)
-        nc.sync.dma_start(xs_table[0:P:ROW_STEP, :].bitcast(I32), x_scales[0].bitcast(I32))
-        nc.sync.dma_start(es_table[0:P:ROW_STEP, :].bitcast(I32), e_scales[0].bitcast(I32))
+        for r in range(SCALE_ROWS):
+            nc.sync.dma_start(xs_table[r:P:QUADRANT, :].bitcast(I32), xs_rows[r].bitcast(I32))
         nc.sync.dma_start(w_raw[1][:], w_rows[:, :, HALF:])
-        nc.sync.dma_start(prior_sb[:], prior)
+        nc.sync.dma_start(pro_sb[:], pro)
+        nc.sync.dma_start(es_table[0:P:ROW_STEP, :].bitcast(I32), e_scales[0].bitcast(I32))
         nc.sync.dma_start(x_table[:].bitcast(I32), x_words[0].rearrange("p n t -> p (n t)").bitcast(I32))
+        nc.sync.dma_start(prior_sb[:], prior)
         nc.sync.dma_start(half_table[HALF_ROW : HALF_ROW + 1, :], half[0:1, :])
+        nc.sync.dma_start(e_table[:].bitcast(I32), e_words[0].rearrange("p n t -> p (n t)").bitcast(I32))
 
         w_bf = keep.tile([P, PACK, P, PACK], BF16, name="w_bf", tag="w_then_x", align_bytes=64)
         for u in range(2):
@@ -81,20 +84,14 @@ def tile_picked_yparz_post_p_kernel(
         def half_list(list_sb, g):
             return list_sb[:, g * HALF // LIST_ROWS : (g + 1) * HALF // LIST_ROWS]
 
-        def gather_scales(name, table, list_sb):
-            spread = keep.tile([P, S], U8, name=f"{name}_spread", align_bytes=64)
-            placed = keep.tile([P, S], U8, name=name, align_bytes=64)
-            nc.vector.tensor_copy(spread[:], table[:].indirect(list_sb[:]))
-            nc.gpsimd.memset(placed[:].bitcast(I32), 0)
-            for r in range(SCALE_ROWS):
-                nc.sync.dma_start(
-                    placed[r:P:QUADRANT, :].bitcast(I32), spread[ROW_STEP * r : P : QUADRANT, :].bitcast(I32)
-                )
-            return placed
-
-        xs = gather_scales("xs", xs_table, offs_sb)
-        nc.sync.dma_start(e_table[:].bitcast(I32), e_words[0].rearrange("p n t -> p (n t)").bitcast(I32))
-        es = gather_scales("es", es_table, pro_sb)
+        xs = keep.tile([P, S], U8, name="xs", align_bytes=64)
+        nc.vector.tensor_copy(xs[:], xs_table[:].indirect(offs_sb[:]))
+        es_spread = keep.tile([P, U], U8, name="es_spread", align_bytes=64)
+        es = keep.tile([P, U], U8, name="es", align_bytes=64)
+        nc.vector.tensor_copy(es_spread[:], es_table[:].indirect(pro_sb[:]))
+        nc.gpsimd.memset(es[:].bitcast(I32), 0)
+        for r in range(SCALE_ROWS):
+            nc.sync.dma_start(es[r:P:QUADRANT, :].bitcast(I32), es_spread[ROW_STEP * r : P : QUADRANT, :].bitcast(I32))
 
         w_codes = keep.tile([P, H], U32, name="w_codes", tag="es_then_w", align_bytes=64)
         w_scales = keep.tile([P, H], U8, name="w_scales", align_bytes=64)

@@ -47,7 +47,7 @@ def tile_picked_yparz_post_p_kernel(
         pro_sb = keep.tile([P, U // LIST_ROWS], U16, name="pro_sb")
         xs_table = keep.tile([P, TABLE], U8, name="xs_table", align_bytes=64)
         es_table = keep.tile([P, TABLE], U8, name="es_table", tag="es_then_w", align_bytes=64)
-        half_table = keep.tile([P, TABLE], F32, name="half_table", tag="half_then_h", align_bytes=64)
+        half_table = keep.tile([P, TABLE], F32, name="half_table", align_bytes=64)
         x_table = tables.tile([P, TABLE], U32, name="x_table", offset=0, align_bytes=64)
         e_table = tables.tile([P, TABLE], U32, name="e_table", offset=WORDS_BYTES, align_bytes=64)
         w_raw = [keep.tile([P, PACK, HALF], F32, name=f"w_raw{u}") for u in range(2)]
@@ -62,18 +62,18 @@ def tile_picked_yparz_post_p_kernel(
         w_rows = w1.rearrange("(p j) c -> p j c", j=PACK)
         xs_rows = x_scales[0].rearrange("(q r) c -> r q c", r=SCALE_ROWS)
         nc.sync.dma_start(offs_sb[:], offs)
+        nc.sync.dma_start(pro_sb[:], pro)
         nc.sync.dma_start(w_raw[0][:], w_rows[:, :, :HALF])
         for r in range(SCALE_ROWS):
             nc.sync.dma_start(xs_table[r:P:QUADRANT, :].bitcast(I32), xs_rows[r].bitcast(I32))
         nc.sync.dma_start(w_raw[1][:], w_rows[:, :, HALF:])
-        nc.sync.dma_start(pro_sb[:], pro)
         nc.sync.dma_start(es_table[0:P:ROW_STEP, :].bitcast(I32), e_scales[0].bitcast(I32))
         nc.sync.dma_start(x_table[:].bitcast(I32), x_words[0].rearrange("p n t -> p (n t)").bitcast(I32))
         nc.sync.dma_start(prior_sb[:], prior)
         nc.sync.dma_start(half_table[HALF_ROW : HALF_ROW + 1, :], half[0:1, :])
         nc.sync.dma_start(e_table[:].bitcast(I32), e_words[0].rearrange("p n t -> p (n t)").bitcast(I32))
 
-        w_bf = keep.tile([P, PACK, P, PACK], BF16, name="w_bf", tag="w_then_x", align_bytes=64)
+        w_bf = keep.tile([P, PACK, P, PACK], BF16, name="w_bf", align_bytes=64)
         for u in range(2):
             nc.scalar.activation(
                 out=w_bf[:].rearrange("p t m j -> p m t j")[:, u * HALF // PACK : (u + 1) * HALF // PACK],
@@ -86,7 +86,7 @@ def tile_picked_yparz_post_p_kernel(
 
         xs = keep.tile([P, S], U8, name="xs", align_bytes=64)
         nc.vector.tensor_copy(xs[:], xs_table[:].indirect(offs_sb[:]))
-        es_spread = keep.tile([P, U], U8, name="es_spread", align_bytes=64)
+        es_spread = keep.tile([P, U], U8, name="es_spread", tag="es_then_h", align_bytes=64)
         es = keep.tile([P, U], U8, name="es", align_bytes=64)
         nc.vector.tensor_copy(es_spread[:], es_table[:].indirect(pro_sb[:]))
         nc.gpsimd.memset(es[:].bitcast(I32), 0)
@@ -98,19 +98,19 @@ def tile_picked_yparz_post_p_kernel(
         nc.vector.quantize_mx(
             out=w_codes[:].bitcast(FP8X4), scales=w_scales[:], in_=w_bf[:].rearrange("p t m j -> p (t m j)")
         )
-        xc = keep.tile([P, S], U32, name="xc", tag="w_then_x", align_bytes=64)
+        xc = keep.tile([P, S], U32, name="xc", align_bytes=64)
         for g in range(2):
             nc.vector.tensor_copy(xc[:, g * HALF : (g + 1) * HALF], x_table[:].indirect(half_list(offs_sb, g)))
 
         prior_rep = keep.tile([P, V, D], F32, name="prior_rep")
         nc.scalar.copy(out=prior_rep[:], in_=prior_sb[:].unsqueeze(2).to_broadcast([P, V, D]))
-        c_row = tables.tile([P, U], F32, name="c_row", offset=0, align_bytes=64)
+        c_row = keep.tile([P, U], F32, name="c_row", align_bytes=64)
         nc.vector.tensor_tensor(
             out=c_row[:], in0=half_table[:].indirect(pro_sb[:]), in1=prior_rep[:].rearrange("p v d -> p (v d)"),
             op=ALU.subtract,
         )
 
-        h_bfs = []
+        h_bf = [keep.tile([P, HALF, PACK], BF16, name=f"h_bf{g}", tag=f"hb{g}", align_bytes=64) for g in range(2)]
         for b in range(BLOCKS):
             samples = slice(b * P, (b + 1) * P)
             h_ps = psum.tile([P, PACK, P], F32, name=f"h_ps{b}", tag=f"h{b}")
@@ -125,9 +125,8 @@ def tile_picked_yparz_post_p_kernel(
                     start=True,
                     stop=True,
                 )
-            h_bf = keep.tile([P, P, PACK], BF16, name=f"h_bf{b}", tag=f"hb{b}", align_bytes=64)
-            nc.scalar.copy(out=h_bf[:], in_=h_ps[:].rearrange("p t n -> p n t"))
-            h_bfs.append(h_bf)
+            g, u = divmod(b, 2)
+            nc.scalar.copy(out=h_bf[g][:, u * P : (u + 1) * P, :], in_=h_ps[:].rearrange("p t n -> p n t"))
 
         c_ps = psum.tile([P, TILES, P], F32, name="c_ps", tag="h0")
         for jb in range(TILES):
@@ -138,19 +137,15 @@ def tile_picked_yparz_post_p_kernel(
         h_scales = [keep.tile([P, HALF], U8, name=f"h_scales{g}", align_bytes=64) for g in range(2)]
 
         def quantise_h(codes, g):
-            for u in range(2):
-                nc.vector.quantize_mx(
-                    out=codes[:, u * P : (u + 1) * P].bitcast(FP8X4),
-                    scales=h_scales[g][:, u * P : (u + 1) * P],
-                    in_=h_bfs[2 * g + u][:].rearrange("p n t -> p (n t)"),
-                )
+            nc.vector.quantize_mx(
+                out=codes[:].bitcast(FP8X4), scales=h_scales[g][:], in_=h_bf[g][:].rearrange("p n t -> p (n t)")
+            )
 
-        h_codes = [keep.tile([P, HALF], U32, name="h_codes0", tag="half_then_h", align_bytes=64)]
+        ec = keep.tile([P, U], U32, name="ec", align_bytes=64)
+        nc.vector.tensor_copy(ec[:], e_table[:].indirect(pro_sb[:]))
+        h_codes = [keep.tile([P, HALF], U32, name="h_codes0", tag="es_then_h", align_bytes=64)]
         quantise_h(h_codes[0], 0)
-        ec = keep.tile([P, U], U32, name="ec", tag="hb1", align_bytes=64)
-        for g in range(2):
-            nc.vector.tensor_copy(ec[:, g * HALF : (g + 1) * HALF], e_table[:].indirect(half_list(pro_sb, g)))
-        h_codes.append(tables.tile([P, HALF], U32, name="h_codes1", offset=WORDS_BYTES, align_bytes=64))
+        h_codes.append(keep.tile([P, HALF], U32, name="h_codes1", tag="hb0", align_bytes=64))
         quantise_h(h_codes[1], 1)
 
         cost_t = [[keep.tile([P, HALF], F32, name=f"cost_t{g}{jb}") for jb in range(TILES)] for g in range(2)]
@@ -184,15 +179,17 @@ def tile_picked_yparz_post_p_kernel(
         early_totals = keep.tile([P, BLOCKS - 1], F32, name="early_totals")
         last_total = keep.tile([P, 1], F32, name="last_total")
         total = [early_totals[:, b : b + 1] for b in range(BLOCKS - 1)] + [last_total[:]]
-        ee = [keep.tile([P, D, V], F32, name=f"ee{b}") for b in range(BLOCKS)]
+        ee = [keep.tile([P, D, V], F32, name=f"ee{b}") for b in range(BLOCKS - 1)]
+        ee.append(keep.tile([P, V, D], F32, name="ee_last"))
         for b in range(BLOCKS):
             g, u = divmod(b, 2)
             cost = psum.tile([P, U], F32, name=f"cost{b}", tag=f"h{b}")
             for jb in range(TILES):
                 nc.tensor.transpose(cost[:, jb * P : (jb + 1) * P], cost_t[g][jb][:, u * P : (u + 1) * P], ident[:])
             nc.vector.tensor_reduce(out=low[b][:], in_=cost[:], axis=AX.X, op=ALU.min)
+            order = "p (v d) -> p v d" if b == BLOCKS - 1 else "p (v d) -> p d v"
             nc.scalar.activation(
-                out=ee[b][:], in_=cost[:].rearrange("p (v d) -> p d v", d=D), func=ACT.Exp, bias=low[b][:], scale=-1.0,
+                out=ee[b][:], in_=cost[:].rearrange(order, d=D), func=ACT.Exp, bias=low[b][:], scale=-1.0,
                 accum_out=total[b],
             )
 
@@ -209,14 +206,14 @@ def tile_picked_yparz_post_p_kernel(
         def add_halves(b, engine):
             engine.tensor_tensor(out=sums[b][:], in0=halves[b][:, 0, :], in1=halves[b][:, 1, :], op=ALU.add)
 
-        add_pairs(0, nc.gpsimd)
-        add_halves(0, nc.gpsimd)
+        add_pairs(0, nc.vector)
+        add_halves(0, nc.vector)
         add_pairs(1, nc.vector)
         nc.vector.reciprocal(out=early_inv[:], in_=early_totals[:])
         add_pairs(2, nc.vector)
         add_halves(1, nc.vector)
         add_halves(2, nc.vector)
-        nc.vector.tensor_reduce(out=sums[3][:], in_=ee[3][:].rearrange("p d v -> p v d"), axis=AX.X, op=ALU.add)
+        nc.vector.tensor_reduce(out=sums[3][:], in_=ee[3][:], axis=AX.X, op=ALU.add)
         nc.vector.reciprocal(out=last_inv[:], in_=last_total[:])
         for b in range(BLOCKS):
             if b < BLOCKS - 1:

@@ -56,6 +56,7 @@ def tile_picked_yparz_post_p_kernel(
         nc.vector.memset(xs_table[:].bitcast(I32), 0)
         nc.vector.memset(es_table[:].bitcast(I32), 0)
         nc.vector.memset(half_table[:], 0.0)
+        nc.vector.memset(prior_sb[:], 0.0)
         ident = keep.tile([P, P], F32, name="ident")
         make_identity(nc, ident[:])
 
@@ -69,7 +70,7 @@ def tile_picked_yparz_post_p_kernel(
         nc.sync.dma_start(w_raw[1][:], w_rows[:, :, HALF:])
         nc.sync.dma_start(es_table[0:P:ROW_STEP, :].bitcast(I32), e_scales[0].bitcast(I32))
         nc.sync.dma_start(x_table[:].bitcast(I32), x_words[0].rearrange("p n t -> p (n t)").bitcast(I32))
-        nc.sync.dma_start(prior_sb[:], prior)
+        nc.sync.dma_start(prior_sb[HALF_ROW : HALF_ROW + 1, :], prior[0:1, :])
         nc.sync.dma_start(half_table[HALF_ROW : HALF_ROW + 1, :], half[0:1, :])
         nc.sync.dma_start(e_table[:].bitcast(I32), e_words[0].rearrange("p n t -> p (n t)").bitcast(I32))
 

@@ -28,6 +28,7 @@ LIST_ROWS = 16
 QUADRANT = 32
 SCALE_ROWS = 4
 HALF = 256
+W_FIRST = 192
 ROW_STEP = 8
 HALF_ROW = 12
 WORDS_BYTES = 4 * TABLE
@@ -50,7 +51,8 @@ def tile_picked_yparz_post_p_kernel(
         half_table = keep.tile([P, TABLE], F32, name="half_table", align_bytes=64)
         x_table = tables.tile([P, TABLE], U32, name="x_table", offset=0, align_bytes=64)
         e_table = tables.tile([P, TABLE], U32, name="e_table", offset=WORDS_BYTES, align_bytes=64)
-        w_raw = [keep.tile([P, PACK, HALF], F32, name=f"w_raw{u}") for u in range(2)]
+        w_cuts = (0, W_FIRST, H)
+        w_raw = [keep.tile([P, PACK, w_cuts[u + 1] - w_cuts[u]], F32, name=f"w_raw{u}") for u in range(2)]
         prior_sb = keep.tile([P, V], F32, name="prior_sb")
 
         nc.vector.memset(xs_table[:].bitcast(I32), 0)
@@ -62,12 +64,12 @@ def tile_picked_yparz_post_p_kernel(
 
         w_rows = w1.rearrange("(p j) c -> p j c", j=PACK)
         xs_rows = x_scales[0].rearrange("(q r) c -> r q c", r=SCALE_ROWS)
+        nc.sync.dma_start(w_raw[0][:], w_rows[:, :, :W_FIRST])
         nc.sync.dma_start(offs_sb[:], offs)
         nc.sync.dma_start(pro_sb[:], pro)
-        nc.sync.dma_start(w_raw[0][:], w_rows[:, :, :HALF])
         for r in range(SCALE_ROWS):
             nc.sync.dma_start(xs_table[r:P:QUADRANT, :].bitcast(I32), xs_rows[r].bitcast(I32))
-        nc.sync.dma_start(w_raw[1][:], w_rows[:, :, HALF:])
+        nc.sync.dma_start(w_raw[1][:], w_rows[:, :, W_FIRST:])
         nc.sync.dma_start(es_table[0:P:ROW_STEP, :].bitcast(I32), e_scales[0].bitcast(I32))
         nc.sync.dma_start(x_table[:].bitcast(I32), x_words[0].rearrange("p n t -> p (n t)").bitcast(I32))
         nc.sync.dma_start(prior_sb[HALF_ROW : HALF_ROW + 1, :], prior[0:1, :])
@@ -77,7 +79,7 @@ def tile_picked_yparz_post_p_kernel(
         w_bf = keep.tile([P, PACK, P, PACK], BF16, name="w_bf", align_bytes=64)
         for u in range(2):
             nc.scalar.activation(
-                out=w_bf[:].rearrange("p t m j -> p m t j")[:, u * HALF // PACK : (u + 1) * HALF // PACK],
+                out=w_bf[:].rearrange("p t m j -> p m t j")[:, w_cuts[u] // PACK : w_cuts[u + 1] // PACK],
                 in_=w_raw[u][:].rearrange("p j (m t) -> p m t j", t=PACK),
                 func=ACT.Copy,
             )

@@ -29,6 +29,7 @@ QUADRANT = 32
 SCALE_ROWS = 4
 HALF = 256
 W_FIRST = 192
+VECTOR_GROUPS = 16
 ROW_STEP = 8
 HALF_ROW = 12
 WORDS_BYTES = 4 * TABLE
@@ -77,12 +78,12 @@ def tile_picked_yparz_post_p_kernel(
         nc.sync.dma_start(e_table[:].bitcast(I32), e_words[0].rearrange("p n t -> p (n t)").bitcast(I32))
 
         w_bf = keep.tile([P, PACK, P, PACK], BF16, name="w_bf", align_bytes=64)
-        for u in range(2):
-            nc.scalar.activation(
-                out=w_bf[:].rearrange("p t m j -> p m t j")[:, w_cuts[u] // PACK : w_cuts[u + 1] // PACK],
-                in_=w_raw[u][:].rearrange("p j (m t) -> p m t j", t=PACK),
-                func=ACT.Copy,
-            )
+        w_out = w_bf[:].rearrange("p t m j -> p m t j")
+        w_in = [w_raw[u][:].rearrange("p j (m t) -> p m t j", t=PACK) for u in range(2)]
+        first, split = W_FIRST // PACK, P - VECTOR_GROUPS
+        nc.scalar.activation(out=w_out[:, :first], in_=w_in[0], func=ACT.Copy)
+        nc.scalar.activation(out=w_out[:, first:split], in_=w_in[1][:, : split - first], func=ACT.Copy)
+        nc.vector.tensor_copy(out=w_out[:, split:], in_=w_in[1][:, split - first :])
 
         def half_list(list_sb, g):
             return list_sb[:, g * HALF // LIST_ROWS : (g + 1) * HALF // LIST_ROWS]

@@ -29,9 +29,10 @@ QUADRANT = 32
 SCALE_ROWS = 4
 HALF = 256
 W_FIRST = 192
-VECTOR_GROUPS = 16
+VECTOR_GROUPS = 24
 ROW_STEP = 8
-HALF_ROW = 12
+ROW_START = 4
+HALF_ROW = 16
 WORDS_BYTES = 4 * TABLE
 FLOPS = 2 * 512 * H * S + 2 * H * S * U
 
@@ -71,15 +72,15 @@ def tile_picked_yparz_post_p_kernel(
         for r in range(SCALE_ROWS):
             nc.sync.dma_start(xs_table[r:P:QUADRANT, :].bitcast(I32), xs_rows[r].bitcast(I32))
         nc.sync.dma_start(w_raw[1][:], w_rows[:, :, W_FIRST:])
-        nc.sync.dma_start(es_table[0:P:ROW_STEP, :].bitcast(I32), e_scales[0].bitcast(I32))
+        nc.sync.dma_start(es_table[ROW_START:P:ROW_STEP, :].bitcast(I32), e_scales[0].bitcast(I32))
         nc.sync.dma_start(x_table[:].bitcast(I32), x_words[0].rearrange("p n t -> p (n t)").bitcast(I32))
         nc.sync.dma_start(prior_sb[HALF_ROW : HALF_ROW + 1, :], prior[0:1, :])
         nc.sync.dma_start(half_table[HALF_ROW : HALF_ROW + 1, :], half[0:1, :])
         nc.sync.dma_start(e_table[:].bitcast(I32), e_words[0].rearrange("p n t -> p (n t)").bitcast(I32))
 
         w_bf = keep.tile([P, PACK, P, PACK], BF16, name="w_bf", align_bytes=64)
-        w_out = w_bf[:].rearrange("p t m j -> p m t j")
-        w_in = [w_raw[u][:].rearrange("p j (m t) -> p m t j", t=PACK) for u in range(2)]
+        w_out = w_bf[:].rearrange("p t m j -> p m j t")
+        w_in = [w_raw[u][:].rearrange("p j (m t) -> p m j t", t=PACK) for u in range(2)]
         first, split = W_FIRST // PACK, P - VECTOR_GROUPS
         nc.scalar.activation(out=w_out[:, :first], in_=w_in[0], func=ACT.Copy)
         nc.scalar.activation(out=w_out[:, first:split], in_=w_in[1][:, : split - first], func=ACT.Copy)
@@ -95,7 +96,7 @@ def tile_picked_yparz_post_p_kernel(
         nc.vector.tensor_copy(es_spread[:], es_table[:].indirect(pro_sb[:]))
         nc.gpsimd.memset(es[:].bitcast(I32), 0)
         for r in range(SCALE_ROWS):
-            nc.sync.dma_start(es[r:P:QUADRANT, :].bitcast(I32), es_spread[ROW_STEP * r : P : QUADRANT, :].bitcast(I32))
+            nc.sync.dma_start(es[r:P:QUADRANT, :].bitcast(I32), es_spread[ROW_START + ROW_STEP * r : P : QUADRANT, :].bitcast(I32))
 
         w_codes = keep.tile([P, H], U32, name="w_codes", tag="es_then_w", align_bytes=64)
         w_scales = keep.tile([P, H], U8, name="w_scales", align_bytes=64)

@@ -28,6 +28,7 @@ LIST_ROWS = 16
 QUADRANT = 32
 SCALE_ROWS = 4
 HALF = 256
+X_PIECES = ((0, 128), (128, 256), (256, 512))
 W_FIRST = 192
 VECTOR_GROUPS = 24
 ROW_STEP = 8
@@ -86,9 +87,6 @@ def tile_picked_yparz_post_p_kernel(
         nc.scalar.activation(out=w_out[:, first:split], in_=w_in[1][:, : split - first], func=ACT.Copy)
         nc.vector.tensor_copy(out=w_out[:, split:], in_=w_in[1][:, split - first :])
 
-        def half_list(list_sb, g):
-            return list_sb[:, g * HALF // LIST_ROWS : (g + 1) * HALF // LIST_ROWS]
-
         xs = keep.tile([P, S], U8, name="xs", align_bytes=64)
         nc.vector.tensor_copy(xs[:], xs_table[:].indirect(offs_sb[:]))
         es_spread = keep.tile([P, U], U8, name="es_spread", tag="es_then_h", align_bytes=64)
@@ -104,8 +102,8 @@ def tile_picked_yparz_post_p_kernel(
             out=w_codes[:].bitcast(FP8X4), scales=w_scales[:], in_=w_bf[:].rearrange("p t m j -> p (t m j)")
         )
         xc = keep.tile([P, S], U32, name="xc", align_bytes=64)
-        for g in range(2):
-            nc.vector.tensor_copy(xc[:, g * HALF : (g + 1) * HALF], x_table[:].indirect(half_list(offs_sb, g)))
+        for lo, hi in X_PIECES:
+            nc.vector.tensor_copy(xc[:, lo:hi], x_table[:].indirect(offs_sb[:, lo // LIST_ROWS : hi // LIST_ROWS]))
 
         prior_rep = keep.tile([P, V, D], F32, name="prior_rep")
         nc.scalar.copy(out=prior_rep[:], in_=prior_sb[:].unsqueeze(2).to_broadcast([P, V, D]))

@@ -35,6 +35,7 @@ ROW_STEP = 8
 ROW_START = 4
 HALF_ROW = 16
 WORDS_BYTES = 4 * TABLE
+H_BYTES = 2 * PACK * HALF
 FLOPS = 2 * 512 * H * S + 2 * H * S * U
 
 
@@ -56,7 +57,7 @@ def tile_picked_yparz_post_p_kernel(
         e_table = tables.tile([P, TABLE], U32, name="e_table", offset=WORDS_BYTES, align_bytes=64)
         w_cuts = (0, W_FIRST, H)
         w_raw = [keep.tile([P, PACK, w_cuts[u + 1] - w_cuts[u]], F32, name=f"w_raw{u}") for u in range(2)]
-        prior_sb = keep.tile([P, V], F32, name="prior_sb")
+        prior_sb = tables.tile([P, V], F32, name="prior_sb", offset=2 * WORDS_BYTES + H_BYTES - HALF, align_bytes=64)
 
         nc.vector.memset(xs_table[:].bitcast(I32), 0)
         nc.vector.memset(es_table[:].bitcast(I32), 0)
@@ -75,8 +76,8 @@ def tile_picked_yparz_post_p_kernel(
         nc.sync.dma_start(w_raw[1][:], w_rows[:, :, W_FIRST:])
         nc.sync.dma_start(es_table[ROW_START:P:ROW_STEP, :].bitcast(I32), e_scales[0].bitcast(I32))
         nc.sync.dma_start(x_table[:].bitcast(I32), x_words[0].rearrange("p n t -> p (n t)").bitcast(I32))
-        nc.sync.dma_start(prior_sb[HALF_ROW : HALF_ROW + 1, :], prior[0:1, :])
         nc.sync.dma_start(half_table[HALF_ROW : HALF_ROW + 1, :], half[0:1, :])
+        nc.sync.dma_start(prior_sb[HALF_ROW : HALF_ROW + 1, :], prior[0:1, :])
         nc.sync.dma_start(e_table[:].bitcast(I32), e_words[0].rearrange("p n t -> p (n t)").bitcast(I32))
 
         w_bf = keep.tile([P, PACK, P, PACK], BF16, name="w_bf", align_bytes=64)
@@ -105,15 +106,26 @@ def tile_picked_yparz_post_p_kernel(
         for lo, hi in X_PIECES:
             nc.vector.tensor_copy(xc[:, lo:hi], x_table[:].indirect(offs_sb[:, lo // LIST_ROWS : hi // LIST_ROWS]))
 
-        prior_rep = keep.tile([P, V, D], F32, name="prior_rep")
-        nc.scalar.copy(out=prior_rep[:], in_=prior_sb[:].unsqueeze(2).to_broadcast([P, V, D]))
-        c_row = keep.tile([P, U], F32, name="c_row", align_bytes=64)
+        fused = U - P
+        half_last = keep.tile([P, P], F32, name="half_last", align_bytes=64)
+        nc.scalar.activation(out=half_last[:], in_=half_table[:].indirect(pro_sb[:, fused // LIST_ROWS :]), func=ACT.Copy)
+        prior_rep = keep.tile([P, fused // D, D], F32, name="prior_rep")
+        nc.scalar.copy(out=prior_rep[:], in_=prior_sb[:, : fused // D].unsqueeze(2).to_broadcast([P, fused // D, D]))
+        prior_neg = keep.tile([P, P // D, D], F32, name="prior_neg")
+        nc.scalar.activation(
+            out=prior_neg[:], in_=prior_sb[:, fused // D :].unsqueeze(2).to_broadcast([P, P // D, D]), func=ACT.Copy,
+            scale=-1.0,
+        )
+        c_row = keep.tile([P, fused], F32, name="c_row", align_bytes=64)
         nc.vector.tensor_tensor(
-            out=c_row[:], in0=half_table[:].indirect(pro_sb[:]), in1=prior_rep[:].rearrange("p v d -> p (v d)"),
-            op=ALU.subtract,
+            out=c_row[:], in0=half_table[:].indirect(pro_sb[:, : fused // LIST_ROWS]),
+            in1=prior_rep[:].rearrange("p v d -> p (v d)"), op=ALU.subtract,
         )
 
-        h_bf = [keep.tile([P, HALF, PACK], BF16, name=f"h_bf{g}", tag=f"hb{g}", align_bytes=64) for g in range(2)]
+        h_bf = [
+            tables.tile([P, HALF, PACK], BF16, name=f"h_bf{g}", offset=2 * WORDS_BYTES + g * H_BYTES, align_bytes=64)
+            for g in range(2)
+        ]
         for b in range(BLOCKS):
             samples = slice(b * P, (b + 1) * P)
             h_ps = psum.tile([P, PACK, P], F32, name=f"h_ps{b}", tag=f"h{b}")
@@ -132,8 +144,12 @@ def tile_picked_yparz_post_p_kernel(
             nc.scalar.copy(out=h_bf[g][:, u * P : (u + 1) * P, :], in_=h_ps[:].rearrange("p t n -> p n t"))
 
         c_ps = psum.tile([P, TILES, P], F32, name="c_ps", tag="h0")
-        for jb in range(TILES):
-            nc.tensor.transpose(c_ps[:, jb, :], c_row[:, jb * P : (jb + 1) * P], ident[:])
+        terms = [(TILES - 1, half_last[:]), (TILES - 1, prior_neg[:].rearrange("p v d -> p (v d)"))]
+        terms += [(jb, c_row[:, jb * P : (jb + 1) * P]) for jb in range(TILES - 1)]
+        for n, (jb, term) in enumerate(terms):
+            nc.tensor.matmul(
+                c_ps[:, jb, :], lhsT=term, rhs=ident[:], is_transpose=True, start=n == 0, stop=n == len(terms) - 1
+            )
         c_col = keep.tile([P, TILES], F32, name="c_col")
         nc.scalar.copy(out=c_col[:], in_=c_ps[:, :, HALF_ROW])
 
@@ -148,7 +164,7 @@ def tile_picked_yparz_post_p_kernel(
         nc.vector.tensor_copy(ec[:], e_table[:].indirect(pro_sb[:]))
         h_codes = [keep.tile([P, HALF], U32, name="h_codes0", tag="es_then_h", align_bytes=64)]
         quantise_h(h_codes[0], 0)
-        h_codes.append(keep.tile([P, HALF], U32, name="h_codes1", tag="hb0", align_bytes=64))
+        h_codes.append(tables.tile([P, HALF], U32, name="h_codes1", offset=2 * WORDS_BYTES, align_bytes=64))
         quantise_h(h_codes[1], 1)
 
         cost_t = [[keep.tile([P, HALF], F32, name=f"cost_t{g}{jb}") for jb in range(TILES)] for g in range(2)]

@@ -57,7 +57,7 @@ def tile_picked_yparz_post_p_kernel(
         e_table = tables.tile([P, TABLE], U32, name="e_table", offset=WORDS_BYTES, align_bytes=64)
         w_cuts = (0, W_FIRST, H)
         w_raw = [keep.tile([P, PACK, w_cuts[u + 1] - w_cuts[u]], F32, name=f"w_raw{u}") for u in range(2)]
-        prior_sb = tables.tile([P, V], F32, name="prior_sb", offset=2 * WORDS_BYTES + H_BYTES - HALF, align_bytes=64)
+        prior_sb = keep.tile([P, V], F32, name="prior_sb")
 
         nc.vector.memset(xs_table[:].bitcast(I32), 0)
         nc.vector.memset(es_table[:].bitcast(I32), 0)
@@ -76,8 +76,8 @@ def tile_picked_yparz_post_p_kernel(
         nc.sync.dma_start(w_raw[1][:], w_rows[:, :, W_FIRST:])
         nc.sync.dma_start(es_table[ROW_START:P:ROW_STEP, :].bitcast(I32), e_scales[0].bitcast(I32))
         nc.sync.dma_start(x_table[:].bitcast(I32), x_words[0].rearrange("p n t -> p (n t)").bitcast(I32))
-        nc.sync.dma_start(half_table[HALF_ROW : HALF_ROW + 1, :], half[0:1, :])
         nc.sync.dma_start(prior_sb[HALF_ROW : HALF_ROW + 1, :], prior[0:1, :])
+        nc.sync.dma_start(half_table[HALF_ROW : HALF_ROW + 1, :], half[0:1, :])
         nc.sync.dma_start(e_table[:].bitcast(I32), e_words[0].rearrange("p n t -> p (n t)").bitcast(I32))
 
         w_bf = keep.tile([P, PACK, P, PACK], BF16, name="w_bf", align_bytes=64)
@@ -107,19 +107,17 @@ def tile_picked_yparz_post_p_kernel(
             nc.vector.tensor_copy(xc[:, lo:hi], x_table[:].indirect(offs_sb[:, lo // LIST_ROWS : hi // LIST_ROWS]))
 
         fused = U - P
-        half_last = keep.tile([P, P], F32, name="half_last", align_bytes=64)
+        prior_rep = keep.tile([P, V, D], F32, name="prior_rep")
+        nc.scalar.copy(out=prior_rep[:], in_=prior_sb[:].unsqueeze(2).to_broadcast([P, V, D]))
+        prior_row = prior_rep[:].rearrange("p v d -> p (v d)")
+        half_last = tables.tile([P, P], F32, name="half_last", offset=2 * WORDS_BYTES + H_BYTES - HALF, align_bytes=64)
         nc.scalar.activation(out=half_last[:], in_=half_table[:].indirect(pro_sb[:, fused // LIST_ROWS :]), func=ACT.Copy)
-        prior_rep = keep.tile([P, fused // D, D], F32, name="prior_rep")
-        nc.scalar.copy(out=prior_rep[:], in_=prior_sb[:, : fused // D].unsqueeze(2).to_broadcast([P, fused // D, D]))
-        prior_neg = keep.tile([P, P // D, D], F32, name="prior_neg")
-        nc.scalar.activation(
-            out=prior_neg[:], in_=prior_sb[:, fused // D :].unsqueeze(2).to_broadcast([P, P // D, D]), func=ACT.Copy,
-            scale=-1.0,
-        )
+        half_neg = keep.tile([P, P], F32, name="half_neg")
+        nc.scalar.activation(out=half_neg[:], in_=half_last[:], func=ACT.Copy, scale=-1.0)
         c_row = keep.tile([P, fused], F32, name="c_row", align_bytes=64)
         nc.vector.tensor_tensor(
             out=c_row[:], in0=half_table[:].indirect(pro_sb[:, : fused // LIST_ROWS]),
-            in1=prior_rep[:].rearrange("p v d -> p (v d)"), op=ALU.subtract,
+            in1=prior_row[:, :fused], op=ALU.subtract,
         )
 
         h_bf = [
@@ -144,14 +142,15 @@ def tile_picked_yparz_post_p_kernel(
             nc.scalar.copy(out=h_bf[g][:, u * P : (u + 1) * P, :], in_=h_ps[:].rearrange("p t n -> p n t"))
 
         c_ps = psum.tile([P, TILES, P], F32, name="c_ps", tag="h0")
-        terms = [(TILES - 1, half_last[:]), (TILES - 1, prior_neg[:].rearrange("p v d -> p (v d)"))]
+        terms = [(TILES - 1, half_neg[:]), (TILES - 1, prior_row[:, fused:])]
         terms += [(jb, c_row[:, jb * P : (jb + 1) * P]) for jb in range(TILES - 1)]
         for n, (jb, term) in enumerate(terms):
             nc.tensor.matmul(
                 c_ps[:, jb, :], lhsT=term, rhs=ident[:], is_transpose=True, start=n == 0, stop=n == len(terms) - 1
             )
         c_col = keep.tile([P, TILES], F32, name="c_col")
-        nc.scalar.copy(out=c_col[:], in_=c_ps[:, :, HALF_ROW])
+        nc.scalar.copy(out=c_col[:, : TILES - 1], in_=c_ps[:, : TILES - 1, HALF_ROW])
+        nc.scalar.activation(out=c_col[:, TILES - 1 :], in_=c_ps[:, TILES - 1 :, HALF_ROW], func=ACT.Copy, scale=-1.0)
 
         h_scales = [keep.tile([P, HALF], U8, name=f"h_scales{g}", align_bytes=64) for g in range(2)]
 
@@ -168,31 +167,39 @@ def tile_picked_yparz_post_p_kernel(
         quantise_h(h_codes[1], 1)
 
         cost_t = [[keep.tile([P, HALF], F32, name=f"cost_t{g}{jb}") for jb in range(TILES)] for g in range(2)]
-        for g in range(2):
-            for pair in range(TILES // 2):
-                y_ps = psum.tile([P, 2, HALF], F32, name=f"y_ps{g}{pair}", tag=f"y{g}{pair}")
-                for u in range(2):
-                    protos = slice((2 * pair + u) * P, (2 * pair + u + 1) * P)
-                    nc.tensor.matmul_mx(
-                        out=y_ps[:, u, :],
-                        lhsT=ec[:, protos].bitcast(FP8X4),
-                        lhsT_scale=es[:, protos],
-                        rhs=h_codes[g][:].bitcast(FP8X4),
-                        rhs_scale=h_scales[g][:],
-                        start=True,
-                        stop=True,
-                    )
-                for u in range(2):
-                    jb = 2 * pair + u
-                    if (g, pair) == (0, 1):
-                        nc.vector.tensor_scalar(
-                            out=cost_t[g][jb][:], in0=y_ps[:, u, :], scalar1=-1.0, scalar2=c_col[:, jb : jb + 1],
-                            op0=ALU.mult, op1=ALU.add,
-                        )
-                    else:
-                        nc.scalar.activation(
-                            out=cost_t[g][jb][:], in_=y_ps[:, u, :], func=ACT.Identity, bias=c_col[:, jb : jb + 1], scale=-1.0
-                        )
+        def multiply(target, g, jb):
+            protos = slice(jb * P, (jb + 1) * P)
+            nc.tensor.matmul_mx(
+                out=target,
+                lhsT=ec[:, protos].bitcast(FP8X4),
+                lhsT_scale=es[:, protos],
+                rhs=h_codes[g][:].bitcast(FP8X4),
+                rhs_scale=h_scales[g][:],
+                start=True,
+                stop=True,
+            )
+
+        def scalar_cost(source, g, jb):
+            nc.scalar.activation(
+                out=cost_t[g][jb][:], in_=source, func=ACT.Identity, bias=c_col[:, jb : jb + 1], scale=-1.0
+            )
+
+        for jb, bank in enumerate(("y0", "y1", "h1", "h2")):
+            y_ps = psum.tile([P, HALF], F32, name=f"y_first{jb}", tag=bank)
+            multiply(y_ps[:], 0, jb)
+            if jb % 2 == 0:
+                nc.vector.tensor_scalar(
+                    out=cost_t[0][jb][:], in0=y_ps[:], scalar1=-1.0, scalar2=c_col[:, jb : jb + 1],
+                    op0=ALU.mult, op1=ALU.add,
+                )
+            else:
+                scalar_cost(y_ps[:], 0, jb)
+        for pair in range(TILES // 2):
+            y_ps = psum.tile([P, 2, HALF], F32, name=f"y_second{pair}", tag=f"y{2 + pair}")
+            for u in range(2):
+                multiply(y_ps[:, u, :], 1, 2 * pair + u)
+            for u in range(2):
+                scalar_cost(y_ps[:, u, :], 1, 2 * pair + u)
 
         low = [keep.tile([P, 1], F32, name=f"low{b}") for b in range(BLOCKS)]
         early_totals = keep.tile([P, BLOCKS - 1], F32, name="early_totals")

@@ -33,7 +33,8 @@ W_FIRST = 192
 VECTOR_GROUPS = 24
 ROW_STEP = 8
 ROW_START = 4
-HALF_ROW = 16
+UPPER = 64
+HALF_ROW = 80
 WORDS_BYTES = 4 * TABLE
 H_BYTES = 2 * PACK * HALF
 FLOPS = 2 * 512 * H * S + 2 * H * S * U
@@ -57,7 +58,7 @@ def tile_picked_yparz_post_p_kernel(
         e_table = tables.tile([P, TABLE], U32, name="e_table", offset=WORDS_BYTES, align_bytes=64)
         w_cuts = (0, W_FIRST, H)
         w_raw = [keep.tile([P, PACK, w_cuts[u + 1] - w_cuts[u]], F32, name=f"w_raw{u}") for u in range(2)]
-        prior_sb = keep.tile([P, V], F32, name="prior_sb")
+        prior_sb = keep.tile([UPPER, P // D], F32, name="prior_sb")
 
         nc.vector.memset(xs_table[:].bitcast(I32), 0)
         nc.vector.memset(es_table[:].bitcast(I32), 0)
@@ -76,7 +77,7 @@ def tile_picked_yparz_post_p_kernel(
         nc.sync.dma_start(w_raw[1][:], w_rows[:, :, W_FIRST:])
         nc.sync.dma_start(es_table[ROW_START:P:ROW_STEP, :].bitcast(I32), e_scales[0].bitcast(I32))
         nc.sync.dma_start(x_table[:].bitcast(I32), x_words[0].rearrange("p n t -> p (n t)").bitcast(I32))
-        nc.sync.dma_start(prior_sb[HALF_ROW : HALF_ROW + 1, :], prior[0:1, :])
+        nc.sync.dma_start(prior_sb[:TILES, :], prior[0].rearrange("(jb a) -> jb a", jb=TILES))
         nc.sync.dma_start(half_table[HALF_ROW : HALF_ROW + 1, :], half[0:1, :])
         nc.sync.dma_start(e_table[:].bitcast(I32), e_words[0].rearrange("p n t -> p (n t)").bitcast(I32))
 
@@ -107,18 +108,16 @@ def tile_picked_yparz_post_p_kernel(
             nc.vector.tensor_copy(xc[:, lo:hi], x_table[:].indirect(offs_sb[:, lo // LIST_ROWS : hi // LIST_ROWS]))
 
         fused = U - P
-        prior_rep = keep.tile([P, V, D], F32, name="prior_rep")
-        nc.scalar.copy(out=prior_rep[:], in_=prior_sb[:].unsqueeze(2).to_broadcast([P, V, D]))
-        prior_row = prior_rep[:].rearrange("p v d -> p (v d)")
         half_last = tables.tile([P, P], F32, name="half_last", offset=2 * WORDS_BYTES + H_BYTES - HALF, align_bytes=64)
         nc.scalar.activation(out=half_last[:], in_=half_table[:].indirect(pro_sb[:, fused // LIST_ROWS :]), func=ACT.Copy)
-        half_neg = keep.tile([P, P], F32, name="half_neg")
-        nc.scalar.activation(out=half_neg[:], in_=half_last[:], func=ACT.Copy, scale=-1.0)
-        c_row = keep.tile([P, fused], F32, name="c_row", align_bytes=64)
-        nc.vector.tensor_tensor(
-            out=c_row[:], in0=half_table[:].indirect(pro_sb[:, : fused // LIST_ROWS]),
-            in1=prior_row[:, :fused], op=ALU.subtract,
+        half_row = keep.tile([P, fused], F32, name="half_row", align_bytes=64)
+        mixed = keep.tile([P, P], F32, name="mixed")
+        nc.scalar.copy(out=mixed[UPPER:, :], in_=half_last[UPPER:, :])
+        nc.scalar.copy(
+            out=mixed[:UPPER, :].rearrange("p (a d) -> p a d", d=D),
+            in_=prior_sb[:].unsqueeze(2).to_broadcast([UPPER, P // D, D]),
         )
+        nc.vector.tensor_copy(half_row[:, :fused], half_table[:].indirect(pro_sb[:, : fused // LIST_ROWS]))
 
         h_bf = [
             tables.tile([P, HALF, PACK], BF16, name=f"h_bf{g}", offset=2 * WORDS_BYTES + g * H_BYTES, align_bytes=64)
@@ -142,15 +141,17 @@ def tile_picked_yparz_post_p_kernel(
             nc.scalar.copy(out=h_bf[g][:, u * P : (u + 1) * P, :], in_=h_ps[:].rearrange("p t n -> p n t"))
 
         c_ps = psum.tile([P, TILES, P], F32, name="c_ps", tag="h0")
-        terms = [(TILES - 1, half_neg[:]), (TILES - 1, prior_row[:, fused:])]
-        terms += [(jb, c_row[:, jb * P : (jb + 1) * P]) for jb in range(TILES - 1)]
-        for n, (jb, term) in enumerate(terms):
-            nc.tensor.matmul(
-                c_ps[:, jb, :], lhsT=term, rhs=ident[:], is_transpose=True, start=n == 0, stop=n == len(terms) - 1
+        rows = [half_row[:, jb * P : (jb + 1) * P] for jb in range(TILES - 1)] + [mixed[:]]
+        for jb in range(TILES):
+            nc.tensor.transpose(c_ps[:, jb, :], rows[jb], ident[:])
+        shift = keep.tile([P, TILES], F32, name="shift")
+        prior_col = keep.tile([P, TILES], F32, name="prior_col")
+        nc.scalar.copy(out=prior_col[:], in_=c_ps[:, TILES - 1, :TILES])
+        for jb in range(TILES):
+            nc.scalar.activation(
+                out=shift[:, jb : jb + 1], in_=c_ps[:, jb, HALF_ROW : HALF_ROW + 1], func=ACT.Identity,
+                bias=prior_col[:, jb : jb + 1], scale=-1.0,
             )
-        c_col = keep.tile([P, TILES], F32, name="c_col")
-        nc.scalar.copy(out=c_col[:, : TILES - 1], in_=c_ps[:, : TILES - 1, HALF_ROW])
-        nc.scalar.activation(out=c_col[:, TILES - 1 :], in_=c_ps[:, TILES - 1 :, HALF_ROW], func=ACT.Copy, scale=-1.0)
 
         h_scales = [keep.tile([P, HALF], U8, name=f"h_scales{g}", align_bytes=64) for g in range(2)]
 
@@ -181,7 +182,7 @@ def tile_picked_yparz_post_p_kernel(
 
         def scalar_cost(source, g, jb):
             nc.scalar.activation(
-                out=cost_t[g][jb][:], in_=source, func=ACT.Identity, bias=c_col[:, jb : jb + 1], scale=-1.0
+                out=cost_t[g][jb][:], in_=source, func=ACT.Identity, bias=shift[:, jb : jb + 1]
             )
 
         for jb, bank in enumerate(("y0", "y1", "h1", "h2")):
@@ -189,8 +190,7 @@ def tile_picked_yparz_post_p_kernel(
             multiply(y_ps[:], 0, jb)
             if jb % 2 == 0:
                 nc.vector.tensor_scalar(
-                    out=cost_t[0][jb][:], in0=y_ps[:], scalar1=-1.0, scalar2=c_col[:, jb : jb + 1],
-                    op0=ALU.mult, op1=ALU.add,
+                    out=cost_t[0][jb][:], in0=y_ps[:], scalar1=shift[:, jb : jb + 1], scalar2=None, op0=ALU.add,
                 )
             else:
                 scalar_cost(y_ps[:], 0, jb)
@@ -212,10 +212,10 @@ def tile_picked_yparz_post_p_kernel(
             cost = psum.tile([P, U], F32, name=f"cost{b}", tag=f"h{b}")
             for jb in range(TILES):
                 nc.tensor.transpose(cost[:, jb * P : (jb + 1) * P], cost_t[g][jb][:, u * P : (u + 1) * P], ident[:])
-            nc.vector.tensor_reduce(out=low[b][:], in_=cost[:], axis=AX.X, op=ALU.min)
+            nc.vector.tensor_reduce(out=low[b][:], in_=cost[:], axis=AX.X, op=ALU.max, negate=True)
             order = "p (v d) -> p v d" if b == BLOCKS - 1 else "p (v d) -> p d v"
             nc.scalar.activation(
-                out=ee[b][:], in_=cost[:].rearrange(order, d=D), func=ACT.Exp, bias=low[b][:], scale=-1.0,
+                out=ee[b][:], in_=cost[:].rearrange(order, d=D), func=ACT.Exp, bias=low[b][:],
                 accum_out=total[b],
             )
 

@@ -37,6 +37,7 @@ UPPER = 64
 HALF_ROW = 80
 WORDS_BYTES = 4 * TABLE
 H_BYTES = 2 * PACK * HALF
+SPREAD_AT = 2 * WORDS_BYTES + 2 * H_BYTES
 FLOPS = 2 * 512 * H * S + 2 * H * S * U
 
 
@@ -91,7 +92,7 @@ def tile_picked_yparz_post_p_kernel(
 
         xs = keep.tile([P, S], U8, name="xs", align_bytes=64)
         nc.vector.tensor_copy(xs[:], xs_table[:].indirect(offs_sb[:]))
-        es_spread = keep.tile([P, U], U8, name="es_spread", tag="es_then_h", align_bytes=64)
+        es_spread = tables.tile([P, U], U8, name="es_spread", offset=SPREAD_AT, align_bytes=64)
         es = keep.tile([P, U], U8, name="es", align_bytes=64)
         nc.vector.tensor_copy(es_spread[:], es_table[:].indirect(pro_sb[:]))
         nc.gpsimd.memset(es[:].bitcast(I32), 0)
@@ -108,16 +109,20 @@ def tile_picked_yparz_post_p_kernel(
             nc.vector.tensor_copy(xc[:, lo:hi], x_table[:].indirect(offs_sb[:, lo // LIST_ROWS : hi // LIST_ROWS]))
 
         fused = U - P
+        half_third = keep.tile([P, P], F32, name="half_third", align_bytes=64)
+        nc.scalar.activation(
+            out=half_third[:], in_=half_table[:].indirect(pro_sb[:, HALF // LIST_ROWS : fused // LIST_ROWS]), func=ACT.Copy
+        )
         half_last = tables.tile([P, P], F32, name="half_last", offset=2 * WORDS_BYTES + H_BYTES - HALF, align_bytes=64)
         nc.scalar.activation(out=half_last[:], in_=half_table[:].indirect(pro_sb[:, fused // LIST_ROWS :]), func=ACT.Copy)
-        half_row = keep.tile([P, fused], F32, name="half_row", align_bytes=64)
+        half_row = keep.tile([P, HALF], F32, name="half_row", align_bytes=64)
         mixed = keep.tile([P, P], F32, name="mixed")
         nc.scalar.copy(out=mixed[UPPER:, :], in_=half_last[UPPER:, :])
         nc.scalar.copy(
             out=mixed[:UPPER, :].rearrange("p (a d) -> p a d", d=D),
             in_=prior_sb[:].unsqueeze(2).to_broadcast([UPPER, P // D, D]),
         )
-        nc.vector.tensor_copy(half_row[:, :fused], half_table[:].indirect(pro_sb[:, : fused // LIST_ROWS]))
+        nc.vector.tensor_copy(half_row[:], half_table[:].indirect(pro_sb[:, : HALF // LIST_ROWS]))
 
         h_bf = [
             tables.tile([P, HALF, PACK], BF16, name=f"h_bf{g}", offset=2 * WORDS_BYTES + g * H_BYTES, align_bytes=64)
@@ -141,7 +146,7 @@ def tile_picked_yparz_post_p_kernel(
             nc.scalar.copy(out=h_bf[g][:, u * P : (u + 1) * P, :], in_=h_ps[:].rearrange("p t n -> p n t"))
 
         c_ps = psum.tile([P, TILES, P], F32, name="c_ps", tag="h0")
-        rows = [half_row[:, jb * P : (jb + 1) * P] for jb in range(TILES - 1)] + [mixed[:]]
+        rows = [half_row[:, jb * P : (jb + 1) * P] for jb in range(2)] + [half_third[:], mixed[:]]
         for jb in range(TILES):
             nc.tensor.transpose(c_ps[:, jb, :], rows[jb], ident[:])
         shift = keep.tile([P, TILES], F32, name="shift")
@@ -153,7 +158,9 @@ def tile_picked_yparz_post_p_kernel(
                 bias=prior_col[:, jb : jb + 1], scale=-1.0,
             )
 
-        h_scales = [keep.tile([P, HALF], U8, name=f"h_scales{g}", align_bytes=64) for g in range(2)]
+        h_scales = [
+            tables.tile([P, HALF], U8, name=f"h_scales{g}", offset=SPREAD_AT + g * HALF, align_bytes=64) for g in range(2)
+        ]
 
         def quantise_h(codes, g):
             nc.vector.quantize_mx(
@@ -162,10 +169,9 @@ def tile_picked_yparz_post_p_kernel(
 
         ec = keep.tile([P, U], U32, name="ec", align_bytes=64)
         nc.vector.tensor_copy(ec[:], e_table[:].indirect(pro_sb[:]))
-        h_codes = [keep.tile([P, HALF], U32, name="h_codes0", tag="es_then_h", align_bytes=64)]
-        quantise_h(h_codes[0], 0)
-        h_codes.append(tables.tile([P, HALF], U32, name="h_codes1", offset=2 * WORDS_BYTES, align_bytes=64))
-        quantise_h(h_codes[1], 1)
+        h_codes = [keep.tile([P, HALF], U32, name=f"h_codes{g}", align_bytes=64) for g in range(2)]
+        for g in range(2):
+            quantise_h(h_codes[g], g)
 
         cost_t = [[keep.tile([P, HALF], F32, name=f"cost_t{g}{jb}") for jb in range(TILES)] for g in range(2)]
         def multiply(target, g, jb):

from contextlib import ExitStack

import concourse.mybir as mybir
from concourse.masks import make_identity

F32 = mybir.dt.float32
BF16 = mybir.dt.bfloat16
I32 = mybir.dt.int32
U32 = mybir.dt.uint32
U16 = mybir.dt.uint16
U8 = mybir.dt.uint8
FP8X4 = mybir.dt.float8_e4m3fn_x4
ALU = mybir.AluOpType
ACT = mybir.ActivationFunctionType
AX = mybir.AxisListType

P = 128
PACK = 4
TABLE = 2048
S = 512
H = 512
U = 512
D = 4
V = 128
BLOCKS = S // P
TILES = U // P
LIST_ROWS = 16
QUADRANT = 32
SCALE_ROWS = 4
HALF = 256
X_PIECES = ((0, 128), (128, 256), (256, 512))
W_FIRST = 192
VECTOR_GROUPS = 24
ROW_STEP = 8
ROW_START = 4
UPPER = 64
HALF_ROW = 80
WORDS_BYTES = 4 * TABLE
H_BYTES = 2 * PACK * HALF
SPREAD_AT = 2 * WORDS_BYTES + 2 * H_BYTES
FLOPS = 2 * 512 * H * S + 2 * H * S * U


def tile_picked_yparz_post_p_kernel(
    tc, x_words, x_scales, w1, e_words, e_scales, half, prior, offs, pro, out
):
    nc = tc.nc
    with ExitStack() as ctx:
        keep = ctx.enter_context(tc.tile_pool(name="keep", bufs=1))
        tables = ctx.enter_context(tc.tile_pool(name="tables", bufs=1))
        psum = ctx.enter_context(tc.psum_pool(name="psum", bufs=1))

        offs_sb = keep.tile([P, S // LIST_ROWS], U16, name="offs_sb")
        pro_sb = keep.tile([P, U // LIST_ROWS], U16, name="pro_sb")
        xs_table = keep.tile([P, TABLE], U8, name="xs_table", align_bytes=64)
        es_table = keep.tile([P, TABLE], U8, name="es_table", tag="es_then_w", align_bytes=64)
        half_table = keep.tile([P, TABLE], F32, name="half_table", align_bytes=64)
        x_table = tables.tile([P, TABLE], U32, name="x_table", offset=0, align_bytes=64)
        e_table = tables.tile([P, TABLE], U32, name="e_table", offset=WORDS_BYTES, align_bytes=64)
        w_cuts = (0, W_FIRST, H)
        w_raw = [keep.tile([P, PACK, w_cuts[u + 1] - w_cuts[u]], F32, name=f"w_raw{u}") for u in range(2)]
        prior_sb = keep.tile([UPPER, P // D], F32, name="prior_sb")

        nc.vector.memset(xs_table[:].bitcast(I32), 0)
        nc.vector.memset(es_table[:].bitcast(I32), 0)
        nc.vector.memset(half_table[:], 0.0)
        nc.vector.memset(prior_sb[:], 0.0)
        ident = keep.tile([P, P], F32, name="ident")
        make_identity(nc, ident[:])

        w_rows = w1.rearrange("(p j) c -> p j c", j=PACK)
        xs_rows = x_scales[0].rearrange("(q r) c -> r q c", r=SCALE_ROWS)
        nc.sync.dma_start(w_raw[0][:], w_rows[:, :, :W_FIRST])
        nc.sync.dma_start(offs_sb[:], offs)
        nc.sync.dma_start(pro_sb[:], pro)
        for r in range(SCALE_ROWS):
            nc.sync.dma_start(xs_table[r:P:QUADRANT, :].bitcast(I32), xs_rows[r].bitcast(I32))
        nc.sync.dma_start(w_raw[1][:], w_rows[:, :, W_FIRST:])
        nc.sync.dma_start(es_table[ROW_START:P:ROW_STEP, :].bitcast(I32), e_scales[0].bitcast(I32))
        nc.sync.dma_start(x_table[:].bitcast(I32), x_words[0].rearrange("p n t -> p (n t)").bitcast(I32))
        nc.sync.dma_start(prior_sb[:TILES, :], prior[0].rearrange("(jb a) -> jb a", jb=TILES))
        nc.sync.dma_start(half_table[HALF_ROW : HALF_ROW + 1, :], half[0:1, :])
        nc.sync.dma_start(e_table[:].bitcast(I32), e_words[0].rearrange("p n t -> p (n t)").bitcast(I32))

        w_bf = keep.tile([P, PACK, P, PACK], BF16, name="w_bf", align_bytes=64)
        w_out = w_bf[:].rearrange("p t m j -> p m j t")
        w_in = [w_raw[u][:].rearrange("p j (m t) -> p m j t", t=PACK) for u in range(2)]
        first, split = W_FIRST // PACK, P - VECTOR_GROUPS
        nc.scalar.activation(out=w_out[:, :first], in_=w_in[0], func=ACT.Copy)
        nc.scalar.activation(out=w_out[:, first:split], in_=w_in[1][:, : split - first], func=ACT.Copy)
        nc.vector.tensor_copy(out=w_out[:, split:], in_=w_in[1][:, split - first :])

        xs = keep.tile([P, S], U8, name="xs", align_bytes=64)
        nc.vector.tensor_copy(xs[:], xs_table[:].indirect(offs_sb[:]))
        es_spread = tables.tile([P, U], U8, name="es_spread", offset=SPREAD_AT, align_bytes=64)
        es = keep.tile([P, U], U8, name="es", align_bytes=64)
        nc.vector.tensor_copy(es_spread[:], es_table[:].indirect(pro_sb[:]))
        nc.gpsimd.memset(es[:].bitcast(I32), 0)
        for r in range(SCALE_ROWS):
            nc.sync.dma_start(es[r:P:QUADRANT, :].bitcast(I32), es_spread[ROW_START + ROW_STEP * r : P : QUADRANT, :].bitcast(I32))

        w_codes = keep.tile([P, H], U32, name="w_codes", tag="es_then_w", align_bytes=64)
        w_scales = keep.tile([P, H], U8, name="w_scales", align_bytes=64)
        nc.vector.quantize_mx(
            out=w_codes[:].bitcast(FP8X4), scales=w_scales[:], in_=w_bf[:].rearrange("p t m j -> p (t m j)")
        )
        xc = keep.tile([P, S], U32, name="xc", align_bytes=64)
        for lo, hi in X_PIECES:
            nc.vector.tensor_copy(xc[:, lo:hi], x_table[:].indirect(offs_sb[:, lo // LIST_ROWS : hi // LIST_ROWS]))

        fused = U - P
        half_third = keep.tile([P, P], F32, name="half_third", align_bytes=64)
        nc.scalar.activation(
            out=half_third[:], in_=half_table[:].indirect(pro_sb[:, HALF // LIST_ROWS : fused // LIST_ROWS]), func=ACT.Copy
        )
        half_last = tables.tile([P, P], F32, name="half_last", offset=2 * WORDS_BYTES + H_BYTES - HALF, align_bytes=64)
        nc.scalar.activation(out=half_last[:], in_=half_table[:].indirect(pro_sb[:, fused // LIST_ROWS :]), func=ACT.Copy)
        half_row = keep.tile([P, HALF], F32, name="half_row", align_bytes=64)
        mixed = keep.tile([P, P], F32, name="mixed")
        nc.scalar.copy(out=mixed[UPPER:, :], in_=half_last[UPPER:, :])
        nc.scalar.copy(
            out=mixed[:UPPER, :].rearrange("p (a d) -> p a d", d=D),
            in_=prior_sb[:].unsqueeze(2).to_broadcast([UPPER, P // D, D]),
        )
        nc.vector.tensor_copy(half_row[:], half_table[:].indirect(pro_sb[:, : HALF // LIST_ROWS]))

        h_bf = [
            tables.tile([P, HALF, PACK], BF16, name=f"h_bf{g}", offset=2 * WORDS_BYTES + g * H_BYTES, align_bytes=64)
            for g in range(2)
        ]
        for b in range(BLOCKS):
            samples = slice(b * P, (b + 1) * P)
            h_ps = psum.tile([P, PACK, P], F32, name=f"h_ps{b}", tag=f"h{b}")
            for t in range(PACK):
                channels = slice(t * P, (t + 1) * P)
                nc.tensor.matmul_mx(
                    out=h_ps[:, t, :],
                    lhsT=w_codes[:, channels].bitcast(FP8X4),
                    lhsT_scale=w_scales[:, channels],
                    rhs=xc[:, samples].bitcast(FP8X4),
                    rhs_scale=xs[:, samples],
                    start=True,
                    stop=True,
                )
            g, u = divmod(b, 2)
            nc.scalar.copy(out=h_bf[g][:, u * P : (u + 1) * P, :], in_=h_ps[:].rearrange("p t n -> p n t"))

        c_ps = psum.tile([P, TILES, P], F32, name="c_ps", tag="h0")
        rows = [half_row[:, jb * P : (jb + 1) * P] for jb in range(2)] + [half_third[:], mixed[:]]
        for jb in range(TILES):
            nc.tensor.transpose(c_ps[:, jb, :], rows[jb], ident[:])
        shift = keep.tile([P, TILES], F32, name="shift")
        prior_col = keep.tile([P, TILES], F32, name="prior_col")
        nc.scalar.copy(out=prior_col[:], in_=c_ps[:, TILES - 1, :TILES])
        for jb in range(TILES):
            nc.scalar.activation(
                out=shift[:, jb : jb + 1], in_=c_ps[:, jb, HALF_ROW : HALF_ROW + 1], func=ACT.Identity,
                bias=prior_col[:, jb : jb + 1], scale=-1.0,
            )

        h_scales = [
            tables.tile([P, HALF], U8, name=f"h_scales{g}", offset=SPREAD_AT + g * HALF, align_bytes=64) for g in range(2)
        ]

        def quantise_h(codes, g):
            nc.vector.quantize_mx(
                out=codes[:].bitcast(FP8X4), scales=h_scales[g][:], in_=h_bf[g][:].rearrange("p n t -> p (n t)")
            )

        ec = keep.tile([P, U], U32, name="ec", align_bytes=64)
        nc.vector.tensor_copy(ec[:], e_table[:].indirect(pro_sb[:]))
        h_codes = [keep.tile([P, HALF], U32, name=f"h_codes{g}", align_bytes=64) for g in range(2)]
        for g in range(2):
            quantise_h(h_codes[g], g)

        cost_t = [[keep.tile([P, HALF], F32, name=f"cost_t{g}{jb}") for jb in range(TILES)] for g in range(2)]
        def multiply(target, g, jb):
            protos = slice(jb * P, (jb + 1) * P)
            nc.tensor.matmul_mx(
                out=target,
                lhsT=ec[:, protos].bitcast(FP8X4),
                lhsT_scale=es[:, protos],
                rhs=h_codes[g][:].bitcast(FP8X4),
                rhs_scale=h_scales[g][:],
                start=True,
                stop=True,
            )

        def scalar_cost(source, g, jb):
            nc.scalar.activation(
                out=cost_t[g][jb][:], in_=source, func=ACT.Identity, bias=shift[:, jb : jb + 1]
            )

        for jb, bank in enumerate(("y0", "y1", "h1", "h2")):
            y_ps = psum.tile([P, HALF], F32, name=f"y_first{jb}", tag=bank)
            multiply(y_ps[:], 0, jb)
            if jb % 2 == 0:
                nc.vector.tensor_scalar(
                    out=cost_t[0][jb][:], in0=y_ps[:], scalar1=shift[:, jb : jb + 1], scalar2=None, op0=ALU.add,
                )
            else:
                scalar_cost(y_ps[:], 0, jb)
        for pair in range(TILES // 2):
            y_ps = psum.tile([P, 2, HALF], F32, name=f"y_second{pair}", tag=f"y{2 + pair}")
            for u in range(2):
                multiply(y_ps[:, u, :], 1, 2 * pair + u)
            for u in range(2):
                scalar_cost(y_ps[:, u, :], 1, 2 * pair + u)

        low = [keep.tile([P, 1], F32, name=f"low{b}") for b in range(BLOCKS)]
        early_totals = keep.tile([P, BLOCKS - 1], F32, name="early_totals")
        last_total = keep.tile([P, 1], F32, name="last_total")
        total = [early_totals[:, b : b + 1] for b in range(BLOCKS - 1)] + [last_total[:]]
        ee = [keep.tile([P, D, V], F32, name=f"ee{b}") for b in range(BLOCKS - 1)]
        ee.append(keep.tile([P, V, D], F32, name="ee_last"))
        for b in range(BLOCKS):
            g, u = divmod(b, 2)
            cost = psum.tile([P, U], F32, name=f"cost{b}", tag=f"h{b}")
            for jb in range(TILES):
                nc.tensor.transpose(cost[:, jb * P : (jb + 1) * P], cost_t[g][jb][:, u * P : (u + 1) * P], ident[:])
            nc.vector.tensor_reduce(out=low[b][:], in_=cost[:], axis=AX.X, op=ALU.max, negate=True)
            order = "p (v d) -> p v d" if b == BLOCKS - 1 else "p (v d) -> p d v"
            nc.scalar.activation(
                out=ee[b][:], in_=cost[:].rearrange(order, d=D), func=ACT.Exp, bias=low[b][:],
                accum_out=total[b],
            )

        early_inv = keep.tile([P, BLOCKS - 1], F32, name="early_inv")
        last_inv = keep.tile([P, 1], F32, name="last_inv")
        inv = [early_inv[:, b : b + 1] for b in range(BLOCKS - 1)] + [last_inv[:]]
        halves = [keep.tile([P, 2, V], F32, name=f"halves{b}") for b in range(BLOCKS - 1)]
        sums = [keep.tile([P, V], F32, name=f"sums{b}") for b in range(BLOCKS)]
        res = [keep.tile([P, V], F32, name=f"res{b}") for b in range(BLOCKS)]

        def add_pairs(b, engine):
            engine.tensor_tensor(out=halves[b][:], in0=ee[b][:, :2, :], in1=ee[b][:, 2:, :], op=ALU.add)

        def add_halves(b, engine):
            engine.tensor_tensor(out=sums[b][:], in0=halves[b][:, 0, :], in1=halves[b][:, 1, :], op=ALU.add)

        add_pairs(0, nc.vector)
        add_halves(0, nc.vector)
        add_pairs(1, nc.vector)
        nc.vector.reciprocal(out=early_inv[:], in_=early_totals[:])
        add_pairs(2, nc.vector)
        add_halves(1, nc.vector)
        add_halves(2, nc.vector)
        nc.vector.tensor_reduce(out=sums[3][:], in_=ee[3][:], axis=AX.X, op=ALU.add)
        nc.vector.reciprocal(out=last_inv[:], in_=last_total[:])
        for b in range(BLOCKS):
            if b < BLOCKS - 1:
                nc.scalar.activation(out=res[b][:], in_=sums[b][:], func=ACT.Copy, scale=inv[b])
            else:
                nc.vector.tensor_scalar(out=res[b][:], in0=sums[b][:], scalar1=inv[b], scalar2=None, op0=ALU.mult)
            nc.sync.dma_start(out[b * P : (b + 1) * P, :], res[b][:])
